import numpy as np
import ml_dtypes


def mxq(x, axis, fmt="e4m3"):
    dtype, down = {"e4m3": (ml_dtypes.float8_e4m3fn, 7), "e5m2": (ml_dtypes.float8_e5m2, 14)}[fmt]
    v = np.moveaxis(np.asarray(x, np.float32).astype(ml_dtypes.bfloat16).astype(np.float64), axis, -1)
    blocks = v.reshape(v.shape[:-1] + (-1, 32))
    amax = np.abs(blocks).max(-1, keepdims=True)
    byte = np.maximum(np.where(amax > 0, np.frexp(amax)[1] - 1 + 127, 0) - down, 1)
    scale = np.exp2(byte - 127.0)
    codes = (blocks / scale).astype(np.float32).astype(dtype).astype(np.float64)
    return np.moveaxis((codes * scale).reshape(v.shape), -1, axis)


WIDE = False


def mx_kscale(k):
    if not WIDE:
        return np.ones(k)
    levels = np.array([10, -10, 5, -5, 0])
    if k % 512:
        return np.exp2(np.random.permutation(np.resize(levels, k // 32))).repeat(32)
    a = np.empty((k // 512, 16))
    for p in range(k // 512):
        a[p, :8] = np.random.permutation(np.resize(levels, 8))
        for g in range(8):
            far = levels[np.abs(levels - a[p, g]) >= 10]
            a[p, g + 8] = far[np.random.randint(len(far))]
    return np.exp2(a.ravel()).repeat(32)


BF16 = ml_dtypes.bfloat16


def bf(x):
    return np.asarray(x, np.float32).astype(BF16)


def f64(x):
    return np.asarray(x).astype(np.float64)


E2M1 = np.array([0.0, 0.5, 1.0, 1.5, 2.0, 3.0, 4.0, 6.0, -0.0, -0.5, -1.0, -1.5, -2.0, -3.0, -4.0, -6.0])


def pack_weight(w, fmt):
    k, n = w.shape
    w = f64(bf(w)).reshape(k // 32, 32, n)
    amax = np.abs(w).max(1)
    if fmt == "e4m3":
        byte = np.frexp(amax)[1] - 1 + 127 - 7
    else:
        mant, ex = np.frexp(amax / 6.0)
        byte = np.where(mant > 0.5, ex, ex - 1) + 127
    byte = np.clip(np.where(amax > 0, byte, 1), 1, 254)
    scaled = (w * np.exp2(127.0 - byte)[:, None, :]).reshape(k, n).astype(np.float32)
    by_word = np.ascontiguousarray(scaled.reshape(k // 512, 128, 4, n).transpose(0, 1, 3, 2))
    if fmt == "e4m3":
        words = by_word.astype(ml_dtypes.float8_e4m3fn).view(np.uint8)
    else:
        c = by_word.astype(ml_dtypes.float4_e2m1fn).view(np.uint8) & 0xF
        words = c[..., 0::2] | (c[..., 1::2] << 4)
    return np.ascontiguousarray(words), np.ascontiguousarray(byte.astype(np.uint8).reshape(k // 512, 16, n))


def unpack_weight(words, scales, fmt):
    g, p, n, _ = words.shape
    if fmt == "e4m3":
        vals = np.ascontiguousarray(words).view(ml_dtypes.float8_e4m3fn).astype(np.float64)
    else:
        nib = np.empty((g, p, n, 4), np.uint8)
        nib[..., 0::2] = words & 0xF
        nib[..., 1::2] = words >> 4
        vals = E2M1[nib]
    vals = vals * np.repeat(np.exp2(scales.astype(np.float64) - 127.0), 8, axis=1)[..., None]
    return vals.transpose(0, 1, 3, 2).reshape(g * 512, n)
def pack4(w):
    words, scales = pack_weight(w, "e2m1")
    return words.reshape(words.shape[0], 128, -1), scales


def unpack4(words, scales):
    return unpack_weight(words.reshape(words.shape[0], 128, -1, 2), scales, "e2m1")


def planes(Y):
    n, m = Y.shape
    b = f64(bf(Y)).reshape(n // 32, 32, m)
    amax = np.abs(b).max(1)
    byte = np.clip(np.where(amax > 0, np.frexp(amax)[1] - 1 + 127 - 7, 1), 1, 254)
    codes = (b * np.exp2(127.0 - byte)[:, None, :]).reshape(n, m).astype(np.float32).astype(ml_dtypes.float8_e4m3fn).view(np.uint8)
    words = codes.reshape(n // 512, 128, 4, m).transpose(0, 1, 3, 2)
    return np.ascontiguousarray(words), np.ascontiguousarray(byte.astype(np.uint8).reshape(n // 512, 16, m))


N, D, M, R, F = 512, 1024, 4, 512, 1024


def setup_inputs():
    s, t = mx_kscale(D), mx_kscale(R)
    x = bf(np.random.standard_normal((N, D)) * s)
    w0_words, w0_scales = pack4(np.random.standard_normal((D, F)) / np.sqrt(D) / s[:, None])
    bases = bf(np.random.standard_normal((M, D, R)) / np.sqrt(D) / s[None, :, None])
    lam = bf(np.random.standard_normal((M, R)) * t[None, :])
    a_words, a_scales = pack4(np.random.standard_normal((R, F)) / np.sqrt(R) / t[:, None])
    gam = bf(np.random.standard_normal((M, F)) * 0.5)
    return {
        "x": x,
        "w0_words": w0_words,
        "w0_scales": w0_scales,
        "bases": bases,
        "lam": lam,
        "a_words": a_words,
        "a_scales": a_scales,
        "gam": gam,
    }


def core(x, w0_words, w0_scales, bases, lam, a_words, a_scales, gam):
    xq = mxq(f64(x), 1, "e4m3")
    h = xq @ mxq(f64(bases), 1, "e4m3")
    hl = h * f64(lam)[:, None, :]
    u = mxq(hl, 2, "e4m3") @ unpack4(a_words, a_scales)
    upd = np.sum(u * f64(gam)[:, None, :], axis=0)
    return (xq @ unpack4(w0_words, w0_scales)) + upd


def reference(x, w0_words, w0_scales, bases, lam, a_words, a_scales, gam):
    R_out = core(x, w0_words, w0_scales, bases, lam, a_words, a_scales, gam)
    words, scales = planes(R_out.T)
    return R_out, words, scales

@@ -1,0 +1,363 @@
+from contextlib import ExitStack
+
+import concourse.mybir as mybir
+from concourse.masks import make_identity
+
+TOK, D, NB, R, F = 512, 1024, 4, 512, 1024
+FLOPS = 2 * TOK * D * R * NB + 2 * TOK * R * F * NB + 2 * TOK * D * F
+
+F32 = mybir.dt.float32
+BF16 = mybir.dt.bfloat16
+U32 = mybir.dt.uint32
+I32 = mybir.dt.int32
+U8 = mybir.dt.uint8
+FP8X4 = mybir.dt.float8_e4m3fn_x4
+FP4X4 = mybir.dt.float4_e2m1fn_x4
+MULT = mybir.AluOpType.mult
+ADD = mybir.AluOpType.add
+COPY = mybir.ActivationFunctionType.Copy
+
+P = 128
+KG = D // 512
+TT = TOK // P
+NJ = F // P
+
+SLOTS = [(0, 0), (1, 0), (0, 1), (2, 0), (1, 1), (3, 0), (2, 1), (3, 1)]
+S_U = {(0, 0): (5,), (1, 0): (1, 3, 5, 7), (2, 0): (1, 3, 5, 7), (3, 0): (0, 1, 3, 5, 7), (0, 1): (), (1, 1): (1, 3, 5, 7), (2, 1): (1, 3, 5, 7), (3, 1): ()}
+VEC_T = (3, (4, 0), 1, 1)
+G_CAST = True
+FIN0 = 2
+IL_LEAD = 1
+XLEAD = 1
+VEC_OUT = set()
+VEC_PL = set()
+
+
+def tile_randlorafullrankbasissum_x2_kernel(
+    tc, x, w0_words, w0_scales, bases, lam, a_words, a_scales, gam, out_0, out_1, out_2
+):
+    nc = tc.nc
+    with ExitStack() as ctx:
+        keep = ctx.enter_context(tc.tile_pool(name="keep", bufs=1))
+        work = ctx.enter_context(tc.tile_pool(name="work", bufs=2))
+        psum = ctx.enter_context(tc.psum_pool(name="psum", bufs=1))
+
+        def bank_h(name, shape, dtype=F32):
+            return psum.tile(shape, dtype, name=name, tag="bank_h", bufs=3)
+
+        def bank_u(name, shape, dtype=F32):
+            return psum.tile(shape, dtype, name=name, tag="bank_u", bufs=5)
+
+        x_sb = keep.tile([P, TT, D], BF16, name="x_sb", align_bytes=64)
+        xg = keep.tile([P, KG, TOK, 4], BF16, name="xg", align_bytes=64)
+        xq = keep.tile([P, KG, TOK], U32, name="xq", align_bytes=64)
+        xs = keep.tile([P, KG, TOK], U8, name="xs", align_bytes=64)
+        braw = [keep.tile([P, KG, 4, R], BF16, name="braw%d" % m, align_bytes=64) for m in range(NB)]
+        bq = [keep.tile([P, KG, R], U32, name="bq%d" % m, align_bytes=64) for m in range(NB)]
+        bs = [keep.tile([P, KG, R], U8, name="bs%d" % m, align_bytes=64) for m in range(NB)]
+        w0 = keep.tile([P, KG, 2 * F], U8, name="w0", align_bytes=64)
+        aw = keep.tile([P, 2 * F], U8, name="aw", align_bytes=64)
+        wsc = keep.tile([P, KG + 1, F], U8, name="wsc", align_bytes=64)
+        vec = keep.tile([P, R + P], BF16, name="vec", align_bytes=64)
+        ident = keep.tile([P, P], F32, name="ident", align_bytes=64)
+        ident_b = keep.tile([P, P], BF16, name="ident_b", align_bytes=64)
+        lam_t = keep.tile([P, NB, 1, 4], F32, name="lam_t", align_bytes=64)
+        gam_t = keep.tile([P, NB * NJ], F32, name="gam_t", align_bytes=64)
+        acc = keep.tile([P, NJ, TOK], F32, name="acc", align_bytes=64)
+        o32 = keep.tile([P, TT, F], F32, name="o32", align_bytes=64)
+        o16 = keep.tile([P, TT, F], BF16, name="o16", align_bytes=64)
+        pg = keep.tile([P, 2, TOK, 4], BF16, name="pg", align_bytes=64)
+        pq = keep.tile([P, 2, TOK], U32, name="pq", align_bytes=64)
+        ps = keep.tile([P, 2, TOK], U8, name="ps", align_bytes=64)
+        part = {}
+        for m, half in sorted(S_U):
+            for j in S_U[(m, half)]:
+                part[(half, j, m)] = keep.tile([P, 256], F32, name="part%d_%d_%d" % (half, j, m), align_bytes=64)
+
+        nc.vector.memset(vec[:], 0.0)
+        nc.gpsimd.memset(wsc[:].rearrange("p a n -> p (a n)").bitcast(I32), 0)
+        make_identity(nc, ident[:])
+        nc.scalar.copy(out=ident_b[:], in_=ident[:])
+        nc.scalar.dma_start(out=vec[0:NB, 0:R], in_=lam[:, :])
+        nc.scalar.dma_start(out=vec[0 : NB * NJ, R : R + P], in_=gam.rearrange("m (j p) -> (m j) p", p=P))
+
+        def load_x(i):
+            nc.sync.dma_start(out=x_sb[:, i, :], in_=x[P * i : P * (i + 1), :])
+
+        def load_b(m):
+            for g in range(KG):
+                nc.sync.dma_start(
+                    out=braw[m][:, g, :, :],
+                    in_=bases[m, 512 * g : 512 * (g + 1), :].rearrange("(p j) r -> p j r", j=4),
+                )
+
+        load_x(0)
+        load_b(0)
+        load_x(1)
+        load_b(1)
+        for q in range(4):
+            nc.sync.dma_start(
+                out=wsc[32 * q : 32 * q + 4, 0:KG, :].bitcast(I32),
+                in_=w0_scales[:, 4 * q : 4 * q + 4, :].rearrange("g q n -> q g n").bitcast(I32),
+            )
+        for q in range(4):
+            nc.sync.dma_start(
+                out=wsc[32 * q : 32 * q + 4, KG, :].bitcast(I32),
+                in_=a_scales[0, 4 * q : 4 * q + 4, :].bitcast(I32),
+            )
+        nc.sync.dma_start(
+            out=w0[:].bitcast(I32),
+            in_=w0_words.rearrange("g p b -> p g b").bitcast(I32),
+        )
+        nc.sync.dma_start(out=aw[:].bitcast(I32), in_=a_words[0].bitcast(I32))
+        load_x(2)
+        load_x(3)
+        load_b(2)
+        load_b(3)
+
+        def interleave(m, g, grouped):
+            v = VEC_T[m]
+            dst = grouped[:].rearrange("p (t c j) -> p t c j", t=4, j=4)
+            srcv = braw[m][:, g, :, :].rearrange("p j (c t) -> p t c j", t=4)
+            if isinstance(v, tuple):
+                v = v[g]
+            if v < 4:
+                nc.scalar.copy(out=dst[:, v:4], in_=srcv[:, v:4])
+            if v > 0:
+                nc.vector.tensor_copy(out=dst[:, 0:v], in_=srcv[:, 0:v])
+
+        def new_grouped(m, g):
+            return work.tile([P, 4 * R], BF16, name="grouped%d_%d" % (m, g), tag="grouped", bufs=6, align_bytes=64)
+
+        def quant_b(m, g, grouped):
+            nc.vector.quantize_mx(out=bq[m][:, g, :].bitcast(FP8X4), scales=bs[m][:, g, :], in_=grouped[:])
+
+        def x_turn(i, engine):
+            words = x_sb[:, i, :].bitcast(F32)
+            bank = bank_u("xt%d" % i, [P, KG, 2, P])
+            for g in range(KG):
+                for u in range(2):
+                    nc.tensor.transpose(bank[:, g, u, :], words[:, 256 * g + u : 256 * (g + 1) : 2], ident[:])
+            dst = xg[:, :, P * i : P * (i + 1), :].rearrange("p g n t -> p g (n t)").bitcast(F32)
+            dst = dst.rearrange("p g (n u) -> p g n u", u=2)
+            engine(out=dst, in_=bank[:].rearrange("p g u n -> p g n u"))
+
+        def quant_x(i0, i1):
+            for g in range(KG):
+                sl = slice(P * i0, P * i1)
+                nc.vector.quantize_mx(
+                    out=xq[:, g, sl].bitcast(FP8X4),
+                    scales=xs[:, g, sl],
+                    in_=xg[:, g, sl, :].rearrange("p n t -> p (n t)"),
+                )
+
+        def stage1(m, i):
+            bank = bank_h("h%d_%d" % (m, i), [P, 4, P])
+            sl = slice(P * i, P * (i + 1))
+            for t in range(4):
+                cols = slice(P * t, P * (t + 1))
+                for g in range(KG):
+                    nc.tensor.matmul_mx(
+                        out=bank[:, t, :],
+                        lhsT=bq[m][:, g, cols].bitcast(FP8X4),
+                        lhsT_scale=bs[m][:, g, cols],
+                        rhs=xq[:, g, sl].bitcast(FP8X4),
+                        rhs_scale=xs[:, g, sl],
+                        start=(g == 0),
+                        stop=(g == KG - 1),
+                    )
+            return bank
+
+        def scale_h(m, i, bank, hl):
+            nc.vector.tensor_tensor(
+                out=hl[:, P * (i % 2) : P * (i % 2 + 1), :],
+                in0=bank[:].rearrange("p t n -> p n t"),
+                in1=lam_t[:, m, :, :].to_broadcast([P, P, 4]),
+                op=MULT,
+            )
+
+        def quant_h(hl, hq, hs):
+            nc.vector.quantize_mx(out=hq[:].bitcast(FP8X4), scales=hs[:], in_=hl[:].rearrange("p n t -> p (n t)"))
+
+        def base(j, half):
+            bank = bank_u("base%d_%d" % (j, half), [P, 256])
+            for n in range(2):
+                sl = slice(256 * half + P * n, 256 * half + P * (n + 1))
+                for g in range(KG):
+                    nc.tensor.matmul_mx(
+                        out=bank[:, P * n : P * (n + 1)],
+                        lhsT=w0[:, g, 256 * j : 256 * (j + 1)].bitcast(FP4X4),
+                        lhsT_scale=wsc[:, g, P * j : P * (j + 1)],
+                        rhs=xq[:, g, sl].bitcast(FP8X4),
+                        rhs_scale=xs[:, g, sl],
+                        start=(g == 0),
+                        stop=(g == KG - 1),
+                    )
+            nc.scalar.copy(out=acc[:, j, 256 * half : 256 * (half + 1)], in_=bank[:])
+
+        def stage2(m, half, j, hq, hs):
+            bank = bank_u("u%d_%d_%d" % (m, half, j), [P, 256])
+            nc.tensor.matmul_mx(
+                out=bank[:],
+                lhsT=aw[:, 256 * j : 256 * (j + 1)].bitcast(FP4X4),
+                lhsT_scale=wsc[:, KG, P * j : P * (j + 1)],
+                rhs=hq[:].bitcast(FP8X4),
+                rhs_scale=hs[:],
+                start=True,
+                stop=True,
+            )
+            col = gam_t[:, NJ * m + j : NJ * m + j + 1]
+            if j in S_U[(m, half)]:
+                nc.scalar.activation(out=part[(half, j, m)][:], in_=bank[:], func=COPY, scale=col)
+            else:
+                sl = slice(256 * half, 256 * (half + 1))
+                nc.vector.scalar_tensor_tensor(
+                    out=acc[:, j, sl], in0=bank[:], scalar=col, in1=acc[:, j, sl], op0=MULT, op1=ADD
+                )
+
+        def parts_of(j, i):
+            half = i // 2
+            sl = slice(P * (i % 2), P * (i % 2 + 1))
+            return [part[k][:, sl] for k in sorted(part) if k[0] == half and k[1] == j] + [acc[:, j, P * i : P * (i + 1)]]
+
+        def out_bank(h, i):
+            bank = bank_u("o%d_%d" % (h, i), [P, 4, P])
+            sl = slice(P * i, P * (i + 1))
+            for jj in range(4):
+                parts = parts_of(4 * h + jj, i)
+                for n, p in enumerate(parts):
+                    nc.tensor.matmul(
+                        bank[:, jj, :],
+                        lhsT=p,
+                        rhs=ident[:],
+                        start=(n == 0),
+                        stop=(n == len(parts) - 1),
+                        is_transpose=True,
+                    )
+            cols = slice(512 * h, 512 * (h + 1))
+            copy = nc.vector.tensor_copy if (h, i) in VEC_OUT else nc.scalar.copy
+            copy(out=o32[:, i, cols], in_=bank[:].rearrange("p j n -> p (j n)"))
+            nc.sync.dma_start(out=out_0[sl, cols], in_=o32[:, i, cols])
+
+        def round_out(h, i):
+            cols = slice(512 * h, 512 * (h + 1))
+            dst = o16[:, i, cols].rearrange("p (u q e) -> p u q e", u=2, e=2)
+            src = o32[:, i, cols].rearrange("p (q u e) -> p u q e", u=2, e=2)
+            if G_CAST and i < 2:
+                nc.gpsimd.tensor_scalar(out=dst, in0=src, scalar1=1.0, scalar2=-0.0, op0=MULT, op1=ADD)
+            else:
+                nc.vector.tensor_copy(out=dst, in_=src)
+
+        def plane_turn(h, ip):
+            bank = bank_h("pt%d_%d" % (h, ip), [P, 2, 2, P])
+            for ii in range(2):
+                words = o16[:, 2 * ip + ii, :].bitcast(F32)
+                for u in range(2):
+                    w = 256 * h + 128 * u
+                    nc.tensor.transpose(bank[:, ii, u, :], words[:, w : w + 128], ident[:])
+            sl = slice(256 * ip, 256 * (ip + 1))
+            dst = pg[:, h, sl, :].rearrange("p n t -> p (n t)").bitcast(F32)
+            dst = dst.rearrange("p (i n u) -> p i n u", i=2, u=2)
+            copy = nc.vector.tensor_copy if (h, ip) in VEC_PL else nc.scalar.copy
+            copy(out=dst, in_=bank[:].rearrange("p i u n -> p i n u"))
+
+        def plane_quant(h, ip):
+            sl = slice(256 * ip, 256 * (ip + 1))
+            nc.vector.quantize_mx(
+                out=pq[:, h, sl].bitcast(FP8X4), scales=ps[:, h, sl], in_=pg[:, h, sl, :].rearrange("p n t -> p (n t)")
+            )
+            nc.sync.dma_start(
+                out=out_1[h].rearrange("p n t -> p (n t)").bitcast(I32)[:, sl], in_=pq[:, h, sl].bitcast(I32)
+            )
+
+        def plane_scales(h):
+            for q in range(4):
+                eng = nc.sync if q % 2 == 0 else nc.scalar
+                eng.dma_start(
+                    out=out_2[h, 4 * q : 4 * q + 4, :].bitcast(I32), in_=ps[32 * q : 32 * q + 4, h, :].bitcast(I32)
+                )
+
+        if True:
+            x_turn(0, nc.scalar.copy)
+            vbank = bank_u("vbank", [P, 5, P], BF16)
+            for t in range(4):
+                nc.tensor.transpose(vbank[:, t, :], vec[:, t:R:4], ident_b[:])
+            nc.tensor.transpose(vbank[:, 4, :], vec[:, R : R + P], ident_b[:])
+            grouped = {}
+
+            def make_grouped(m, g):
+                grouped[(m, g)] = new_grouped(m, g)
+                interleave(m, g, grouped[(m, g)])
+
+            make_grouped(0, 0)
+            quant_x(0, 1)
+            make_grouped(0, 1)
+            quant_b(0, 0, grouped[(0, 0)])
+            nc.scalar.copy(
+                out=lam_t[:].rearrange("p m o t -> p m (o t)"), in_=vbank[:, 0:4, 0:NB].rearrange("p t m -> p m t")
+            )
+            nc.scalar.copy(out=gam_t[:], in_=vbank[:, 4, 0 : NB * NJ])
+            x_turn(1, nc.scalar.copy)
+            quant_b(0, 1, grouped[(0, 1)])
+            quant_x(1, 2)
+
+            hls = {}
+            IL = {}
+            QB = {}
+            for m in range(1, NB):
+                f = SLOTS.index((m, 0))
+                IL[f - IL_LEAD] = [(m, 0), (m, 1)]
+                QB[f - 1] = [(m, 0), (m, 1)]
+            xslot = SLOTS.index((0, 1)) - XLEAD
+            a_end = SLOTS.index((3, 0))
+            FIN = {}
+            for k in range(6):
+                FIN.setdefault(min(a_end + FIN0 + k // 2, len(SLOTS)), []).append(k)
+
+            def finish(step, half):
+                seq = [(h, 2 * half + ii) for h in range(2) for ii in range(2)]
+                if step < 4:
+                    out_bank(*seq[step])
+                if 1 <= step <= 4:
+                    round_out(*seq[step - 1])
+                if step in (2, 4):
+                    plane_turn(step // 2 - 1, half)
+                if step in (3, 5):
+                    plane_quant((step - 3) // 2, half)
+
+            for n in range(len(SLOTS) + 1):
+                cur = SLOTS[n] if n < len(SLOTS) else None
+                prev = SLOTS[n - 1] if n > 0 else None
+                if cur:
+                    hl = work.tile([P, 256, 4], BF16, name="hl%d" % n, tag="hl", bufs=2, align_bytes=64)
+                    hq = work.tile([P, 256], U32, name="hq%d" % n, tag="hq", bufs=2, align_bytes=64)
+                    hs = work.tile([P, 256], U8, name="hs%d" % n, tag="hs", bufs=2, align_bytes=64)
+                    hls[n] = (hl, hq, hs)
+                for i in range(2):
+                    if cur:
+                        bank = stage1(cur[0], 2 * cur[1] + i)
+                    for k, mg in enumerate(IL.get(n, ())):
+                        if k == i:
+                            make_grouped(*mg)
+                    if n == xslot:
+                        x_turn(2 + i, nc.scalar.copy)
+                    if cur:
+                        scale_h(cur[0], 2 * cur[1] + i, bank, hls[n][0])
+                    if prev:
+                        for j in range(4 * i, 4 * i + 4):
+                            if prev[0] == 0:
+                                base(j, prev[1])
+                            stage2(prev[0], prev[1], j, hls[n - 1][1], hls[n - 1][2])
+                    if n == xslot and i == 1:
+                        quant_x(2, 4)
+                    for k, step in enumerate(FIN.get(n, ())):
+                        if min(k // max(1, len(FIN[n]) // 2), 1) == i:
+                            finish(step, 0)
+                for mg in QB.get(n, ()):
+                    quant_b(*mg, grouped[mg])
+                if cur:
+                    quant_h(*hls[n])
+            for step in range(6):
+                finish(step, 1)
+            plane_scales(0)
+            plane_scales(1)

@@ -22,15 +22,14 @@ KG = D // 512
 TT = TOK // P
 NJ = F // P
 
-SLOTS = [(0, 0), (1, 0), (0, 1), (2, 0), (1, 1), (3, 0), (2, 1), (3, 1)]
-S_U = {(0, 0): (5,), (1, 0): (1, 3, 5, 7), (2, 0): (1, 3, 5, 7), (3, 0): (0, 1, 3, 5, 7), (0, 1): (), (1, 1): (1, 3, 5, 7), (2, 1): (1, 3, 5, 7), (3, 1): ()}
-VEC_T = (3, (4, 0), 1, 1)
-G_CAST = True
-FIN0 = 2
-IL_LEAD = 1
-XLEAD = 1
-VEC_OUT = set()
-VEC_PL = set()
+S_U = {(2, j) for j in range(NJ)} | {(1, j) for j in (1, 3, 5, 7)}
+VEC_T = (2, 2, 1, 0)
+G_CAST = ()
+VEC_OUT = ()
+VEC_PL = (3,)
+VEC_BASE = ()
+PH2 = 1
+MANUAL = False
 
 
 def tile_randlorafullrankbasissum_x2_kernel(
@@ -69,10 +68,12 @@ def tile_randlorafullrankbasissum_x2_kernel(
         pg = keep.tile([P, 2, TOK, 4], BF16, name="pg", align_bytes=64)
         pq = keep.tile([P, 2, TOK], U32, name="pq", align_bytes=64)
         ps = keep.tile([P, 2, TOK], U8, name="ps", align_bytes=64)
+        hl = [keep.tile([P, TOK, 4], BF16, name="hl%d" % m, align_bytes=64) for m in range(NB)]
+        hq = [keep.tile([P, TOK], U32, name="hq%d" % m, align_bytes=64) for m in range(NB)]
+        hs = [keep.tile([P, TOK], U8, name="hs%d" % m, align_bytes=64) for m in range(NB)]
         part = {}
-        for m, half in sorted(S_U):
-            for j in S_U[(m, half)]:
-                part[(half, j, m)] = keep.tile([P, 256], F32, name="part%d_%d_%d" % (half, j, m), align_bytes=64)
+        for m, j in sorted(S_U):
+            part[(m, j)] = keep.tile([P, TOK], F32, name="part%d_%d" % (m, j), align_bytes=64)
 
         nc.vector.memset(vec[:], 0.0)
         nc.gpsimd.memset(wsc[:].rearrange("p a n -> p (a n)").bitcast(I32), 0)
@@ -94,6 +95,8 @@ def tile_randlorafullrankbasissum_x2_kernel(
         load_x(0)
         load_b(0)
         load_x(1)
+        load_x(2)
+        load_x(3)
         load_b(1)
         for q in range(4):
             nc.sync.dma_start(
@@ -110,29 +113,29 @@ def tile_randlorafullrankbasissum_x2_kernel(
             in_=w0_words.rearrange("g p b -> p g b").bitcast(I32),
         )
         nc.sync.dma_start(out=aw[:].bitcast(I32), in_=a_words[0].bitcast(I32))
-        load_x(2)
-        load_x(3)
         load_b(2)
         load_b(3)
 
-        def interleave(m, g, grouped):
+        grouped = {}
+
+        def interleave(m, g):
+            tile_ = work.tile([P, 4 * R], BF16, name="grouped%d_%d" % (m, g), tag="grouped", bufs=6, align_bytes=64)
+            grouped[(m, g)] = tile_
             v = VEC_T[m]
-            dst = grouped[:].rearrange("p (t c j) -> p t c j", t=4, j=4)
-            srcv = braw[m][:, g, :, :].rearrange("p j (c t) -> p t c j", t=4)
             if isinstance(v, tuple):
                 v = v[g]
+            dst = tile_[:].rearrange("p (t c i j) -> p c t i j", t=4, i=2, j=4)
+            srcv = braw[m][:, g, :, :].rearrange("p j (c i t) -> p c t i j", i=2, t=4)
+            cut = 16 * v
             if v < 4:
-                nc.scalar.copy(out=dst[:, v:4], in_=srcv[:, v:4])
+                nc.scalar.copy(out=dst[:, cut:64], in_=srcv[:, cut:64])
             if v > 0:
-                nc.vector.tensor_copy(out=dst[:, 0:v], in_=srcv[:, 0:v])
+                nc.vector.tensor_copy(out=dst[:, 0:cut], in_=srcv[:, 0:cut])
 
-        def new_grouped(m, g):
-            return work.tile([P, 4 * R], BF16, name="grouped%d_%d" % (m, g), tag="grouped", bufs=6, align_bytes=64)
+        def quant_b(m, g):
+            nc.vector.quantize_mx(out=bq[m][:, g, :].bitcast(FP8X4), scales=bs[m][:, g, :], in_=grouped[(m, g)][:])
 
-        def quant_b(m, g, grouped):
-            nc.vector.quantize_mx(out=bq[m][:, g, :].bitcast(FP8X4), scales=bs[m][:, g, :], in_=grouped[:])
-
-        def x_turn(i, engine):
+        def x_turn(i):
             words = x_sb[:, i, :].bitcast(F32)
             bank = bank_u("xt%d" % i, [P, KG, 2, P])
             for g in range(KG):
@@ -140,7 +143,7 @@ def tile_randlorafullrankbasissum_x2_kernel(
                     nc.tensor.transpose(bank[:, g, u, :], words[:, 256 * g + u : 256 * (g + 1) : 2], ident[:])
             dst = xg[:, :, P * i : P * (i + 1), :].rearrange("p g n t -> p g (n t)").bitcast(F32)
             dst = dst.rearrange("p g (n u) -> p g n u", u=2)
-            engine(out=dst, in_=bank[:].rearrange("p g u n -> p g n u"))
+            nc.scalar.copy(out=dst, in_=bank[:].rearrange("p g u n -> p g n u"))
 
         def quant_x(i0, i1):
             for g in range(KG):
@@ -166,84 +169,79 @@ def tile_randlorafullrankbasissum_x2_kernel(
                         start=(g == 0),
                         stop=(g == KG - 1),
                     )
-            return bank
-
-        def scale_h(m, i, bank, hl):
             nc.vector.tensor_tensor(
-                out=hl[:, P * (i % 2) : P * (i % 2 + 1), :],
+                out=hl[m][:, sl, :],
                 in0=bank[:].rearrange("p t n -> p n t"),
                 in1=lam_t[:, m, :, :].to_broadcast([P, P, 4]),
                 op=MULT,
             )
 
-        def quant_h(hl, hq, hs):
-            nc.vector.quantize_mx(out=hq[:].bitcast(FP8X4), scales=hs[:], in_=hl[:].rearrange("p n t -> p (n t)"))
+        def quant_h(m, half):
+            sl = slice(256 * half, 256 * (half + 1))
+            nc.vector.quantize_mx(
+                out=hq[m][:, sl].bitcast(FP8X4), scales=hs[m][:, sl], in_=hl[m][:, sl, :].rearrange("p n t -> p (n t)")
+            )
 
-        def base(j, half):
-            bank = bank_u("base%d_%d" % (j, half), [P, 256])
-            for n in range(2):
-                sl = slice(256 * half + P * n, 256 * half + P * (n + 1))
-                for g in range(KG):
-                    nc.tensor.matmul_mx(
-                        out=bank[:, P * n : P * (n + 1)],
-                        lhsT=w0[:, g, 256 * j : 256 * (j + 1)].bitcast(FP4X4),
-                        lhsT_scale=wsc[:, g, P * j : P * (j + 1)],
-                        rhs=xq[:, g, sl].bitcast(FP8X4),
-                        rhs_scale=xs[:, g, sl],
-                        start=(g == 0),
-                        stop=(g == KG - 1),
-                    )
-            nc.scalar.copy(out=acc[:, j, 256 * half : 256 * (half + 1)], in_=bank[:])
+        def base(j):
+            bank = bank_u("base%d" % j, [P, TOK])
+            for g in range(KG):
+                nc.tensor.matmul_mx(
+                    out=bank[:],
+                    lhsT=w0[:, g, 256 * j : 256 * (j + 1)].bitcast(FP4X4),
+                    lhsT_scale=wsc[:, g, P * j : P * (j + 1)],
+                    rhs=xq[:, g, :].bitcast(FP8X4),
+                    rhs_scale=xs[:, g, :],
+                    start=(g == 0),
+                    stop=(g == KG - 1),
+                )
+            copy = nc.vector.tensor_copy if j in VEC_BASE else nc.scalar.copy
+            copy(out=acc[:, j, :], in_=bank[:])
 
-        def stage2(m, half, j, hq, hs):
-            bank = bank_u("u%d_%d_%d" % (m, half, j), [P, 256])
+        def stage2(m, j):
+            bank = bank_u("u%d_%d" % (m, j), [P, TOK])
             nc.tensor.matmul_mx(
                 out=bank[:],
                 lhsT=aw[:, 256 * j : 256 * (j + 1)].bitcast(FP4X4),
                 lhsT_scale=wsc[:, KG, P * j : P * (j + 1)],
-                rhs=hq[:].bitcast(FP8X4),
-                rhs_scale=hs[:],
+                rhs=hq[m][:].bitcast(FP8X4),
+                rhs_scale=hs[m][:],
                 start=True,
                 stop=True,
             )
             col = gam_t[:, NJ * m + j : NJ * m + j + 1]
-            if j in S_U[(m, half)]:
-                nc.scalar.activation(out=part[(half, j, m)][:], in_=bank[:], func=COPY, scale=col)
+            if (m, j) in S_U:
+                nc.scalar.activation(out=part[(m, j)][:], in_=bank[:], func=COPY, scale=col)
             else:
-                sl = slice(256 * half, 256 * (half + 1))
                 nc.vector.scalar_tensor_tensor(
-                    out=acc[:, j, sl], in0=bank[:], scalar=col, in1=acc[:, j, sl], op0=MULT, op1=ADD
+                    out=acc[:, j, :], in0=bank[:], scalar=col, in1=acc[:, j, :], op0=MULT, op1=ADD
                 )
 
-        def parts_of(j, i):
-            half = i // 2
-            sl = slice(P * (i % 2), P * (i % 2 + 1))
-            return [part[k][:, sl] for k in sorted(part) if k[0] == half and k[1] == j] + [acc[:, j, P * i : P * (i + 1)]]
-
-        def out_bank(h, i):
-            bank = bank_u("o%d_%d" % (h, i), [P, 4, P])
-            sl = slice(P * i, P * (i + 1))
-            for jj in range(4):
-                parts = parts_of(4 * h + jj, i)
-                for n, p in enumerate(parts):
+        def out_bank(j):
+            bank = bank_h("o%d" % j, [P, TT, P])
+            parts = [part[key][:] for key in sorted(part) if key[1] == j] + [acc[:, j, :]]
+            for i in range(TT):
+                for n, piece in enumerate(parts):
                     nc.tensor.matmul(
-                        bank[:, jj, :],
-                        lhsT=p,
+                        bank[:, i, :],
+                        lhsT=piece[:, P * i : P * (i + 1)],
                         rhs=ident[:],
                         start=(n == 0),
                         stop=(n == len(parts) - 1),
                         is_transpose=True,
                     )
-            cols = slice(512 * h, 512 * (h + 1))
-            copy = nc.vector.tensor_copy if (h, i) in VEC_OUT else nc.scalar.copy
-            copy(out=o32[:, i, cols], in_=bank[:].rearrange("p j n -> p (j n)"))
-            nc.sync.dma_start(out=out_0[sl, cols], in_=o32[:, i, cols])
+            cols = slice(P * j, P * (j + 1))
+            copy = nc.vector.tensor_copy if j in VEC_OUT else nc.scalar.copy
+            copy(out=o32[:, :, cols], in_=bank[:])
 
-        def round_out(h, i):
-            cols = slice(512 * h, 512 * (h + 1))
-            dst = o16[:, i, cols].rearrange("p (u q e) -> p u q e", u=2, e=2)
-            src = o32[:, i, cols].rearrange("p (q u e) -> p u q e", u=2, e=2)
-            if G_CAST and i < 2:
+        def store(j0, j1):
+            cols = slice(P * j0, P * j1)
+            nc.sync.dma_start(out=out_0[:, cols].rearrange("(i p) f -> p i f", p=P), in_=o32[:, :, cols])
+
+        def round_out(j):
+            h, jj = j // 4, j % 4
+            dst = o16[:].rearrange("p i (h u q e) -> p i h u q e", h=2, u=2, e=2)[:, :, h, :, 32 * jj : 32 * (jj + 1), :]
+            src = o32[:, :, P * j : P * (j + 1)].rearrange("p i (q u e) -> p i u q e", u=2, e=2)
+            if j in G_CAST:
                 nc.gpsimd.tensor_scalar(out=dst, in0=src, scalar1=1.0, scalar2=-0.0, op0=MULT, op1=ADD)
             else:
                 nc.vector.tensor_copy(out=dst, in_=src)
@@ -258,7 +256,7 @@ def tile_randlorafullrankbasissum_x2_kernel(
             sl = slice(256 * ip, 256 * (ip + 1))
             dst = pg[:, h, sl, :].rearrange("p n t -> p (n t)").bitcast(F32)
             dst = dst.rearrange("p (i n u) -> p i n u", i=2, u=2)
-            copy = nc.vector.tensor_copy if (h, ip) in VEC_PL else nc.scalar.copy
+            copy = nc.vector.tensor_copy if 2 * h + ip in VEC_PL else nc.scalar.copy
             copy(out=dst, in_=bank[:].rearrange("p i u n -> p i n u"))
 
         def plane_quant(h, ip):
@@ -277,87 +275,86 @@ def tile_randlorafullrankbasissum_x2_kernel(
                     out=out_2[h, 4 * q : 4 * q + 4, :].bitcast(I32), in_=ps[32 * q : 32 * q + 4, h, :].bitcast(I32)
                 )
 
-        if True:
-            x_turn(0, nc.scalar.copy)
+        def compute():
+            x_turn(0)
             vbank = bank_u("vbank", [P, 5, P], BF16)
             for t in range(4):
                 nc.tensor.transpose(vbank[:, t, :], vec[:, t:R:4], ident_b[:])
             nc.tensor.transpose(vbank[:, 4, :], vec[:, R : R + P], ident_b[:])
-            grouped = {}
-
-            def make_grouped(m, g):
-                grouped[(m, g)] = new_grouped(m, g)
-                interleave(m, g, grouped[(m, g)])
-
-            make_grouped(0, 0)
+            interleave(0, 0)
             quant_x(0, 1)
-            make_grouped(0, 1)
-            quant_b(0, 0, grouped[(0, 0)])
+            interleave(0, 1)
+            quant_b(0, 0)
             nc.scalar.copy(
                 out=lam_t[:].rearrange("p m o t -> p m (o t)"), in_=vbank[:, 0:4, 0:NB].rearrange("p t m -> p m t")
             )
             nc.scalar.copy(out=gam_t[:], in_=vbank[:, 4, 0 : NB * NJ])
-            x_turn(1, nc.scalar.copy)
-            quant_b(0, 1, grouped[(0, 1)])
+            x_turn(1)
+            quant_b(0, 1)
             quant_x(1, 2)
-
-            hls = {}
-            IL = {}
-            QB = {}
-            for m in range(1, NB):
-                f = SLOTS.index((m, 0))
-                IL[f - IL_LEAD] = [(m, 0), (m, 1)]
-                QB[f - 1] = [(m, 0), (m, 1)]
-            xslot = SLOTS.index((0, 1)) - XLEAD
-            a_end = SLOTS.index((3, 0))
-            FIN = {}
-            for k in range(6):
-                FIN.setdefault(min(a_end + FIN0 + k // 2, len(SLOTS)), []).append(k)
-
-            def finish(step, half):
-                seq = [(h, 2 * half + ii) for h in range(2) for ii in range(2)]
-                if step < 4:
-                    out_bank(*seq[step])
-                if 1 <= step <= 4:
-                    round_out(*seq[step - 1])
-                if step in (2, 4):
-                    plane_turn(step // 2 - 1, half)
-                if step in (3, 5):
-                    plane_quant((step - 3) // 2, half)
-
-            for n in range(len(SLOTS) + 1):
-                cur = SLOTS[n] if n < len(SLOTS) else None
-                prev = SLOTS[n - 1] if n > 0 else None
-                if cur:
-                    hl = work.tile([P, 256, 4], BF16, name="hl%d" % n, tag="hl", bufs=2, align_bytes=64)
-                    hq = work.tile([P, 256], U32, name="hq%d" % n, tag="hq", bufs=2, align_bytes=64)
-                    hs = work.tile([P, 256], U8, name="hs%d" % n, tag="hs", bufs=2, align_bytes=64)
-                    hls[n] = (hl, hq, hs)
-                for i in range(2):
-                    if cur:
-                        bank = stage1(cur[0], 2 * cur[1] + i)
-                    for k, mg in enumerate(IL.get(n, ())):
-                        if k == i:
-                            make_grouped(*mg)
-                    if n == xslot:
-                        x_turn(2 + i, nc.scalar.copy)
-                    if cur:
-                        scale_h(cur[0], 2 * cur[1] + i, bank, hls[n][0])
-                    if prev:
-                        for j in range(4 * i, 4 * i + 4):
-                            if prev[0] == 0:
-                                base(j, prev[1])
-                            stage2(prev[0], prev[1], j, hls[n - 1][1], hls[n - 1][2])
-                    if n == xslot and i == 1:
-                        quant_x(2, 4)
-                    for k, step in enumerate(FIN.get(n, ())):
-                        if min(k // max(1, len(FIN[n]) // 2), 1) == i:
-                            finish(step, 0)
-                for mg in QB.get(n, ()):
-                    quant_b(*mg, grouped[mg])
-                if cur:
-                    quant_h(*hls[n])
-            for step in range(6):
-                finish(step, 1)
-            plane_scales(0)
+            x_turn(2)
+            x_turn(3)
+            quant_x(2, 4)
+            for s in range(NB + 1):
+                for i in range(4):
+                    if s < NB:
+                        stage1(s, i)
+                    if s + 1 < NB and i < 2:
+                        interleave(s + 1, i)
+                    if s == 1:
+                        base(i)
+                    if s > 0:
+                        stage2(s - 1, i)
+                    if s < NB and i == 2:
+                        quant_h(s, 0)
+                    if s + 1 < NB and i > 1:
+                        quant_b(s + 1, i - 2)
+                if s < NB:
+                    quant_h(s, 1)
+                if PH2 and s > 1:
+                    for j in range(4, 4 + PH2):
+                        if s == 2:
+                            base(j)
+                        stage2(s - 2, j)
+            for j in range(4 + PH2, 8):
+                base(j)
+            for pair in ((4, 5), (6, 7)):
+                for m in range(NB):
+                    for j in pair:
+                        if j >= 4 + PH2 or m == NB - 1:
+                            stage2(m, j)
+                    if pair[0] == 4:
+                        out_bank(m)
+                        if m in (1, 3):
+                            store(m - 1, m + 1)
+                        round_out(m)
+                    if pair[0] == 6:
+                        if m == 0:
+                            plane_turn(0, 0)
+                            plane_turn(0, 1)
+                        if m == 1:
+                            plane_quant(0, 0)
+                            plane_quant(0, 1)
+                            plane_scales(0)
+                        if m == 2:
+                            out_bank(4)
+                            round_out(4)
+                        if m == 3:
+                            out_bank(5)
+                            store(4, 6)
+                            round_out(5)
+            for j in (6, 7):
+                out_bank(j)
+                store(j, j + 1)
+                round_out(j)
+            plane_turn(1, 0)
+            plane_turn(1, 1)
+            plane_quant(1, 0)
+            plane_quant(1, 1)
             plane_scales(1)
+
+        if MANUAL:
+            with tc.manual_schedule():
+                compute()
+        else:
+            compute()

@@ -22,14 +22,19 @@ KG = D // 512
 TT = TOK // P
 NJ = F // P
 
-S_U = {(2, j) for j in range(NJ)} | {(1, j) for j in (1, 3, 5, 7)}
-VEC_T = (2, 2, 1, 0)
+S_U = {(1, j) for j in range(NJ)} | {(2, j) for j in (1, 3, 5, 7)}
+VEC_T = (3, 2, 2, 0)
 G_CAST = ()
+G_ADD = True
 VEC_OUT = ()
 VEC_PL = (3,)
 VEC_BASE = ()
-PH2 = 1
-MANUAL = False
+BANKS = (2, 6)
+TUNE = {}
+DEFAULT_TUNE = dict(
+    ov=45, psr=475, tr=75, ga=950, hop=80, sem=100, raw=150, switch=100, slack=0, bias={"o": 3000, "qb": -500, "rd": 500, "to": -1500},
+    at=dict(x=(3400, 4700, 5150, 5600), vec=4000, b=(2950, 4300, 6500, 7400, 10400, 11300, 12200, 13100), w=9000, a=9500),
+)
 
 
 def tile_randlorafullrankbasissum_x2_kernel(
@@ -42,10 +47,10 @@ def tile_randlorafullrankbasissum_x2_kernel(
         psum = ctx.enter_context(tc.psum_pool(name="psum", bufs=1))
 
         def bank_h(name, shape, dtype=F32):
-            return psum.tile(shape, dtype, name=name, tag="bank_h", bufs=3)
+            return psum.tile(shape, dtype, name=name, tag="bank_h", bufs=BANKS[0])
 
         def bank_u(name, shape, dtype=F32):
-            return psum.tile(shape, dtype, name=name, tag="bank_u", bufs=5)
+            return psum.tile(shape, dtype, name=name, tag="bank_u", bufs=BANKS[1])
 
         x_sb = keep.tile([P, TT, D], BF16, name="x_sb", align_bytes=64)
         xg = keep.tile([P, KG, TOK, 4], BF16, name="xg", align_bytes=64)
@@ -76,61 +81,58 @@ def tile_randlorafullrankbasissum_x2_kernel(
             part[(m, j)] = keep.tile([P, TOK], F32, name="part%d_%d" % (m, j), align_bytes=64)
 
         nc.vector.memset(vec[:], 0.0)
-        nc.gpsimd.memset(wsc[:].rearrange("p a n -> p (a n)").bitcast(I32), 0)
         make_identity(nc, ident[:])
+        nc.gpsimd.memset(wsc[:].rearrange("p a n -> p (a n)").bitcast(I32), 0)
         nc.scalar.copy(out=ident_b[:], in_=ident[:])
-        nc.scalar.dma_start(out=vec[0:NB, 0:R], in_=lam[:, :])
-        nc.scalar.dma_start(out=vec[0 : NB * NJ, R : R + P], in_=gam.rearrange("m (j p) -> (m j) p", p=P))
 
         def load_x(i):
             nc.sync.dma_start(out=x_sb[:, i, :], in_=x[P * i : P * (i + 1), :])
 
-        def load_b(m):
-            for g in range(KG):
-                nc.sync.dma_start(
-                    out=braw[m][:, g, :, :],
-                    in_=bases[m, 512 * g : 512 * (g + 1), :].rearrange("(p j) r -> p j r", j=4),
-                )
-
-        load_x(0)
-        load_b(0)
-        load_x(1)
-        load_x(2)
-        load_x(3)
-        load_b(1)
-        for q in range(4):
+        def load_b(m, g):
             nc.sync.dma_start(
+                out=braw[m][:, g, :, :],
+                in_=bases[m, 512 * g : 512 * (g + 1), :].rearrange("(p j) r -> p j r", j=4),
+            )
+
+        load_b(0, 0)
+        load_x(0)
+        load_b(0, 1)
+        nc.scalar.dma_start(out=vec[0:NB, 0:R], in_=lam[:, :])
+        nc.scalar.dma_start(out=vec[0 : NB * NJ, R : R + P], in_=gam.rearrange("m (j p) -> (m j) p", p=P))
+        for q in range(4):
+            nc.gpsimd.dma_start(
                 out=wsc[32 * q : 32 * q + 4, 0:KG, :].bitcast(I32),
                 in_=w0_scales[:, 4 * q : 4 * q + 4, :].rearrange("g q n -> q g n").bitcast(I32),
             )
         for q in range(4):
-            nc.sync.dma_start(
+            nc.gpsimd.dma_start(
                 out=wsc[32 * q : 32 * q + 4, KG, :].bitcast(I32),
                 in_=a_scales[0, 4 * q : 4 * q + 4, :].bitcast(I32),
             )
+        load_x(1)
+        load_x(2)
+        load_x(3)
+        load_b(1, 0)
+        load_b(1, 1)
         nc.sync.dma_start(
             out=w0[:].bitcast(I32),
             in_=w0_words.rearrange("g p b -> p g b").bitcast(I32),
         )
         nc.sync.dma_start(out=aw[:].bitcast(I32), in_=a_words[0].bitcast(I32))
-        load_b(2)
-        load_b(3)
+        load_b(2, 0)
+        load_b(2, 1)
+        load_b(3, 0)
+        load_b(3, 1)
 
         grouped = {}
 
-        def interleave(m, g):
-            tile_ = work.tile([P, 4 * R], BF16, name="grouped%d_%d" % (m, g), tag="grouped", bufs=6, align_bytes=64)
-            grouped[(m, g)] = tile_
-            v = VEC_T[m]
-            if isinstance(v, tuple):
-                v = v[g]
-            dst = tile_[:].rearrange("p (t c i j) -> p c t i j", t=4, i=2, j=4)
-            srcv = braw[m][:, g, :, :].rearrange("p j (c i t) -> p c t i j", i=2, t=4)
-            cut = 16 * v
-            if v < 4:
-                nc.scalar.copy(out=dst[:, cut:64], in_=srcv[:, cut:64])
-            if v > 0:
-                nc.vector.tensor_copy(out=dst[:, 0:cut], in_=srcv[:, 0:cut])
+        def interleave(m, g, c0, c1, copy):
+            if (m, g) not in grouped:
+                tile_ = work.tile([P, 4 * R], BF16, name="grouped%d_%d" % (m, g), tag="grouped", bufs=8, align_bytes=64)
+                grouped[(m, g)] = tile_
+            dst = grouped[(m, g)][:].rearrange("p (t c i j) -> p c t i j", t=4, i=2, j=4)
+            src = braw[m][:, g, :, :].rearrange("p j (c i t) -> p c t i j", i=2, t=4)
+            copy(out=dst[:, c0:c1], in_=src[:, c0:c1])
 
         def quant_b(m, g):
             nc.vector.quantize_mx(out=bq[m][:, g, :].bitcast(FP8X4), scales=bs[m][:, g, :], in_=grouped[(m, g)][:])
@@ -141,6 +143,10 @@ def tile_randlorafullrankbasissum_x2_kernel(
             for g in range(KG):
                 for u in range(2):
                     nc.tensor.transpose(bank[:, g, u, :], words[:, 256 * g + u : 256 * (g + 1) : 2], ident[:])
+            banks[("x", i)] = bank
+
+        def take_x(i):
+            bank = banks[("x", i)]
             dst = xg[:, :, P * i : P * (i + 1), :].rearrange("p g n t -> p g (n t)").bitcast(F32)
             dst = dst.rearrange("p g (n u) -> p g n u", u=2)
             nc.scalar.copy(out=dst, in_=bank[:].rearrange("p g u n -> p g n u"))
@@ -153,6 +159,8 @@ def tile_randlorafullrankbasissum_x2_kernel(
                     scales=xs[:, g, sl],
                     in_=xg[:, g, sl, :].rearrange("p n t -> p (n t)"),
                 )
+
+        banks = {}
 
         def stage1(m, i):
             bank = bank_h("h%d_%d" % (m, i), [P, 4, P])
@@ -169,9 +177,12 @@ def tile_randlorafullrankbasissum_x2_kernel(
                         start=(g == 0),
                         stop=(g == KG - 1),
                     )
+            banks[(m, i)] = bank
+
+        def scale_h(m, i):
             nc.vector.tensor_tensor(
-                out=hl[m][:, sl, :],
-                in0=bank[:].rearrange("p t n -> p n t"),
+                out=hl[m][:, P * i : P * (i + 1), :],
+                in0=banks[(m, i)][:].rearrange("p t n -> p n t"),
                 in1=lam_t[:, m, :, :].to_broadcast([P, P, 4]),
                 op=MULT,
             )
@@ -194,8 +205,11 @@ def tile_randlorafullrankbasissum_x2_kernel(
                     start=(g == 0),
                     stop=(g == KG - 1),
                 )
+            banks[("base", j)] = bank
+
+        def take_base(j):
             copy = nc.vector.tensor_copy if j in VEC_BASE else nc.scalar.copy
-            copy(out=acc[:, j, :], in_=bank[:])
+            copy(out=acc[:, j, :], in_=banks[("base", j)][:])
 
         def stage2(m, j):
             bank = bank_u("u%d_%d" % (m, j), [P, TOK])
@@ -208,6 +222,10 @@ def tile_randlorafullrankbasissum_x2_kernel(
                 start=True,
                 stop=True,
             )
+            banks[("u", m, j)] = bank
+
+        def take_u(m, j):
+            bank = banks[("u", m, j)]
             col = gam_t[:, NJ * m + j : NJ * m + j + 1]
             if (m, j) in S_U:
                 nc.scalar.activation(out=part[(m, j)][:], in_=bank[:], func=COPY, scale=col)
@@ -218,7 +236,9 @@ def tile_randlorafullrankbasissum_x2_kernel(
 
         def out_bank(j):
             bank = bank_h("o%d" % j, [P, TT, P])
-            parts = [part[key][:] for key in sorted(part) if key[1] == j] + [acc[:, j, :]]
+            parts = [acc[:, j, :]]
+            if not G_ADD:
+                parts = [part[mj][:] for mj in sorted(part) if mj[1] == j] + parts
             for i in range(TT):
                 for n, piece in enumerate(parts):
                     nc.tensor.matmul(
@@ -229,9 +249,15 @@ def tile_randlorafullrankbasissum_x2_kernel(
                         stop=(n == len(parts) - 1),
                         is_transpose=True,
                     )
+            banks[("o", j)] = bank
+
+        def add_u(m, j):
+            nc.gpsimd.tensor_tensor(out=acc[:, j, :], in0=acc[:, j, :], in1=part[(m, j)][:], op=ADD)
+
+        def take_out(j):
             cols = slice(P * j, P * (j + 1))
             copy = nc.vector.tensor_copy if j in VEC_OUT else nc.scalar.copy
-            copy(out=o32[:, :, cols], in_=bank[:])
+            copy(out=o32[:, :, cols], in_=banks[("o", j)][:])
 
         def store(j0, j1):
             cols = slice(P * j0, P * j1)
@@ -253,6 +279,10 @@ def tile_randlorafullrankbasissum_x2_kernel(
                 for u in range(2):
                     w = 256 * h + 128 * u
                     nc.tensor.transpose(bank[:, ii, u, :], words[:, w : w + 128], ident[:])
+            banks[("p", h, ip)] = bank
+
+        def take_plane(h, ip):
+            bank = banks[("p", h, ip)]
             sl = slice(256 * ip, 256 * (ip + 1))
             dst = pg[:, h, sl, :].rearrange("p n t -> p (n t)").bitcast(F32)
             dst = dst.rearrange("p (i n u) -> p i n u", i=2, u=2)
@@ -275,86 +305,144 @@ def tile_randlorafullrankbasissum_x2_kernel(
                     out=out_2[h, 4 * q : 4 * q + 4, :].bitcast(I32), in_=ps[32 * q : 32 * q + 4, h, :].bitcast(I32)
                 )
 
-        def compute():
-            x_turn(0)
+        def turn_vectors():
             vbank = bank_u("vbank", [P, 5, P], BF16)
             for t in range(4):
                 nc.tensor.transpose(vbank[:, t, :], vec[:, t:R:4], ident_b[:])
             nc.tensor.transpose(vbank[:, 4, :], vec[:, R : R + P], ident_b[:])
-            interleave(0, 0)
-            quant_x(0, 1)
-            interleave(0, 1)
-            quant_b(0, 0)
+            banks["v"] = vbank
+
+        def take_vectors():
+            vbank = banks["v"]
             nc.scalar.copy(
                 out=lam_t[:].rearrange("p m o t -> p m (o t)"), in_=vbank[:, 0:4, 0:NB].rearrange("p t m -> p m t")
             )
             nc.scalar.copy(out=gam_t[:], in_=vbank[:, 4, 0 : NB * NJ])
-            x_turn(1)
-            quant_b(0, 1)
-            quant_x(1, 2)
-            x_turn(2)
-            x_turn(3)
-            quant_x(2, 4)
-            for s in range(NB + 1):
-                for i in range(4):
-                    if s < NB:
-                        stage1(s, i)
-                    if s + 1 < NB and i < 2:
-                        interleave(s + 1, i)
-                    if s == 1:
-                        base(i)
-                    if s > 0:
-                        stage2(s - 1, i)
-                    if s < NB and i == 2:
-                        quant_h(s, 0)
-                    if s + 1 < NB and i > 1:
-                        quant_b(s + 1, i - 2)
-                if s < NB:
-                    quant_h(s, 1)
-                if PH2 and s > 1:
-                    for j in range(4, 4 + PH2):
-                        if s == 2:
-                            base(j)
-                        stage2(s - 2, j)
-            for j in range(4 + PH2, 8):
-                base(j)
-            for pair in ((4, 5), (6, 7)):
-                for m in range(NB):
-                    for j in pair:
-                        if j >= 4 + PH2 or m == NB - 1:
-                            stage2(m, j)
-                    if pair[0] == 4:
-                        out_bank(m)
-                        if m in (1, 3):
-                            store(m - 1, m + 1)
-                        round_out(m)
-                    if pair[0] == 6:
-                        if m == 0:
-                            plane_turn(0, 0)
-                            plane_turn(0, 1)
-                        if m == 1:
-                            plane_quant(0, 0)
-                            plane_quant(0, 1)
-                            plane_scales(0)
-                        if m == 2:
-                            out_bank(4)
-                            round_out(4)
-                        if m == 3:
-                            out_bank(5)
-                            store(4, 6)
-                            round_out(5)
-            for j in (6, 7):
-                out_bank(j)
-                store(j, j + 1)
-                round_out(j)
-            plane_turn(1, 0)
-            plane_turn(1, 1)
-            plane_quant(1, 0)
-            plane_quant(1, 1)
-            plane_scales(1)
 
-        if MANUAL:
-            with tc.manual_schedule():
-                compute()
-        else:
-            compute()
+        ops = {}
+
+        def op(name, engine, weight, deps, fn, takes=None, frees=None, at=0):
+            ops[name] = (engine, weight, tuple(deps), fn, takes, frees, at)
+
+        T = dict(DEFAULT_TUNE)
+        T.update(TUNE)
+        ov, psr, tr = T["ov"], T["psr"], T["tr"]
+        at = T["at"]
+        for i in range(TT):
+            op(("xt", i), "P", 6 * tr, (), lambda i=i: x_turn(i), takes="u", at=at["x"][i])
+            op(("tx", i), "S", psr, [("xt", i)], lambda i=i: take_x(i), frees="u")
+            op(("qx", i), "V", 250 + 2 * ov, [("tx", i)], lambda i=i: quant_x(i, i + 1))
+        op("vt", "P", 400, (), turn_vectors, takes="u", at=at["vec"])
+        op("tv", "S", 100, ["vt"], take_vectors, frees="u")
+        for m in range(NB):
+            for g in range(KG):
+                cut = 16 * VEC_T[m]
+                deps = []
+                if cut > 0:
+                    deps.append(("iv", m, g))
+                    op(deps[-1], "V", 17.5 * cut + ov, (), lambda m=m, g=g, cut=cut: interleave(m, g, 0, cut, nc.vector.tensor_copy), at=at["b"][2 * m + g])
+                if cut < 64:
+                    deps.append(("is", m, g))
+                    op(deps[-1], "S", 32 * (64 - cut) + ov, (), lambda m=m, g=g, cut=cut: interleave(m, g, cut, 64, nc.scalar.copy), at=at["b"][2 * m + g])
+                op(("qb", m, g), "V", 463 + ov, deps, lambda m=m, g=g: quant_b(m, g))
+            for i in range(TT):
+                op(("s1", m, i), "P", 492, [("qb", m, 0), ("qb", m, 1), ("qx", i)], lambda m=m, i=i: stage1(m, i), takes="h")
+                op(("tt", m, i), "V", psr, [("s1", m, i), "tv"], lambda m=m, i=i: scale_h(m, i), frees="h")
+            for half in range(2):
+                op(("qh", m, half), "V", 237 + ov, [("tt", m, 2 * half), ("tt", m, 2 * half + 1)], lambda m=m, half=half: quant_h(m, half))
+        for j in range(NJ):
+            op(("base", j), "P", 440, [("qx", i) for i in range(TT)], lambda j=j: base(j), takes="u", at=at["w"])
+            op(("tb", j), "V" if j in VEC_BASE else "S", psr, [("base", j)], lambda j=j: take_base(j), frees="u")
+            last, waits, parts = ("tb", j), [], 1
+            for m in range(NB):
+                op(("s2", m, j), "P", 220, [("qh", m, 0), ("qh", m, 1)], lambda m=m, j=j: stage2(m, j), takes="u", at=at["a"])
+                if (m, j) in S_U:
+                    op(("tu", m, j), "S", psr, [("s2", m, j)], lambda m=m, j=j: take_u(m, j), frees="u")
+                    if G_ADD:
+                        op(("ga", m, j), "G", T["ga"], [("tu", m, j), last], lambda m=m, j=j: add_u(m, j))
+                        last = ("ga", m, j)
+                    else:
+                        waits.append(("tu", m, j))
+                        parts += 1
+                else:
+                    op(("tu", m, j), "V", psr, [("s2", m, j), last], lambda m=m, j=j: take_u(m, j), frees="u")
+                    last = ("tu", m, j)
+            op(("o", j), "P", 4 * parts * tr, waits + [last], lambda j=j: out_bank(j), takes="h")
+            op(("to", j), "V" if j in VEC_OUT else "S", psr, [("o", j)], lambda j=j: take_out(j), frees="h")
+            op(("rd", j), "G" if j in G_CAST else "V", 600 if j in G_CAST else 215 + ov, [("to", j)], lambda j=j: round_out(j))
+        for j in range(0, NJ, 2):
+            op(("st", j), "D", 10, [("to", j), ("to", j + 1)], lambda j=j: store(j, j + 2))
+        for h in range(2):
+            for ip in range(2):
+                op(("pt", h, ip), "P", 4 * tr, [("rd", j) for j in range(4 * h, 4 * h + 4)], lambda h=h, ip=ip: plane_turn(h, ip), takes="h")
+                op(("tp", h, ip), "V" if 2 * h + ip in VEC_PL else "S", psr, [("pt", h, ip)], lambda h=h, ip=ip: take_plane(h, ip), frees="h")
+                op(("pq", h, ip), "V", 237 + ov, [("tp", h, ip)], lambda h=h, ip=ip: plane_quant(h, ip))
+            op(("ps", h), "D", 10, [("pq", h, 0), ("pq", h, 1)], lambda h=h: plane_scales(h))
+
+        def order_ops():
+            after = {n: [] for n in ops}
+            for n in ops:
+                for dep in ops[n][2]:
+                    after[dep].append(n)
+            way = {}
+            for n in reversed(list(ops)):
+                stack = [n]
+                while stack:
+                    top = stack[-1]
+                    todo = [a for a in after[top] if a not in way]
+                    if todo:
+                        stack.extend(todo)
+                    else:
+                        way[stack.pop()] = ops[top][1] + T["hop"] + max([way[a] for a in after[top]] + [0])
+            for n in way:
+                kind = n[0] if isinstance(n, tuple) else n
+                way[n] += T["bias"].get(kind, 0)
+            free = {"h": [0] * BANKS[0], "u": [0] * BANKS[1]}
+            clock = {"P": 0, "V": 0, "S": 0, "G": 0, "D": 0}
+            ready = {n: ops[n][6] for n in ops}
+            left = {n: len(ops[n][2]) for n in ops}
+            open_ops = [n for n in ops if left[n] == 0]
+            order, kind_before = [], None
+            while open_ops:
+                best = None
+                for e in clock:
+                    starts = []
+                    for n in open_ops:
+                        if ops[n][0] == e and (ops[n][4] is None or free[ops[n][4]]):
+                            t = max(clock[e], ready[n])
+                            if ops[n][4]:
+                                t = max(t, min(free[ops[n][4]]))
+                            starts.append((t, n))
+                    if starts:
+                        soon = min([t for t, n in starts]) + T["slack"]
+                        t, n = max([(way[n], t, str(n), n) for t, n in starts if t <= soon])[1::2]
+                        if best is None or t < best[0]:
+                            best = (t, n)
+                t, n = best
+                e, weight, deps, fn, takes, frees, arrival = ops[n]
+                if takes:
+                    free[takes].remove(min(free[takes]))
+                if e == "P":
+                    k = n[0] in ("xt", "o", "pt") or n == "vt"
+                    if kind_before is not None and k != kind_before:
+                        t += T["switch"]
+                    kind_before = k
+                end = t + weight
+                clock[e] = end
+                if frees:
+                    free[frees].append(end + T["sem"])
+                open_ops.remove(n)
+                order.append(n)
+                for a in after[n]:
+                    lag = T["sem"] + (100 if e == "P" else 0)
+                    if ops[a][0] == e:
+                        lag = T["raw"] if e == "V" else 0
+                    ready[a] = max(ready[a], end + lag)
+                    left[a] -= 1
+                    if left[a] == 0:
+                        open_ops.append(a)
+            return order
+
+        with tc.manual_schedule():
+            for n in order_ops():
+                ops[n][3]()

@@ -23,17 +23,20 @@ TT = TOK // P
 NJ = F // P
 
 S_U = {(1, j) for j in range(NJ)} | {(2, j) for j in (1, 3, 5, 7)}
-VEC_T = (3, 2, 2, 0)
-G_CAST = ()
-G_ADD = True
+VEC_T = ((48, 48), (64, 0), (32, 0), (0, 0))
+QB_SPLIT = (0, 1)
+RD_SPLIT = (6,)
+PQ_SPLIT = (1,)
+G_CAST = (0,)
+G_U = S_U
 VEC_OUT = ()
-VEC_PL = (3,)
+VEC_PL = ()
 VEC_BASE = ()
-BANKS = (2, 6)
+BANKS = (3, 5)
 TUNE = {}
 DEFAULT_TUNE = dict(
-    ov=45, psr=475, tr=75, ga=950, hop=80, sem=100, raw=150, switch=100, slack=0, bias={"o": 3000, "qb": -500, "rd": 500, "to": -1500},
-    at=dict(x=(3400, 4700, 5150, 5600), vec=4000, b=(2950, 4300, 6500, 7400, 10400, 11300, 12200, 13100), w=9000, a=9500),
+    ov=100, psr=533, tr=75, ga=950, hop=80, sem=100, raw=150, switch=100, slack=60, bias={"qb": -1000, "qh": -500, "s2": 500, "tb": -500, "to": -4000},
+    at=dict(x=(3400, 4700, 5150, 5600), vec=4000, b=(2950, 4300, 6700, 7700, 10700, 11600, 12500, 13300), w=9200, a=9900),
 )
 
 
@@ -53,9 +56,9 @@ def tile_randlorafullrankbasissum_x2_kernel(
             return psum.tile(shape, dtype, name=name, tag="bank_u", bufs=BANKS[1])
 
         x_sb = keep.tile([P, TT, D], BF16, name="x_sb", align_bytes=64)
-        xg = keep.tile([P, KG, TOK, 4], BF16, name="xg", align_bytes=64)
-        xq = keep.tile([P, KG, TOK], U32, name="xq", align_bytes=64)
-        xs = keep.tile([P, KG, TOK], U8, name="xs", align_bytes=64)
+        xg = keep.tile([P, TT, KG, P, 4], BF16, name="xg", align_bytes=64)
+        xq = keep.tile([P, TT, KG, P], U32, name="xq", align_bytes=64)
+        xs = keep.tile([P, TT, KG, P], U8, name="xs", align_bytes=64)
         braw = [keep.tile([P, KG, 4, R], BF16, name="braw%d" % m, align_bytes=64) for m in range(NB)]
         bq = [keep.tile([P, KG, R], U32, name="bq%d" % m, align_bytes=64) for m in range(NB)]
         bs = [keep.tile([P, KG, R], U8, name="bs%d" % m, align_bytes=64) for m in range(NB)]
@@ -94,48 +97,55 @@ def tile_randlorafullrankbasissum_x2_kernel(
                 in_=bases[m, 512 * g : 512 * (g + 1), :].rearrange("(p j) r -> p j r", j=4),
             )
 
+        def load_w0_scales(q):
+            nc.sync.dma_start(
+                out=wsc[32 * q : 32 * q + 4, 0:KG, :].bitcast(I32),
+                in_=w0_scales[:, 4 * q : 4 * q + 4, :].rearrange("g q n -> q g n").bitcast(I32),
+            )
+
+        def load_a_scales(q):
+            nc.sync.dma_start(
+                out=wsc[32 * q : 32 * q + 4, KG, :].bitcast(I32), in_=a_scales[0, 4 * q : 4 * q + 4, :].bitcast(I32)
+            )
+
         load_b(0, 0)
         load_x(0)
         load_b(0, 1)
         nc.scalar.dma_start(out=vec[0:NB, 0:R], in_=lam[:, :])
         nc.scalar.dma_start(out=vec[0 : NB * NJ, R : R + P], in_=gam.rearrange("m (j p) -> (m j) p", p=P))
-        for q in range(4):
-            nc.gpsimd.dma_start(
-                out=wsc[32 * q : 32 * q + 4, 0:KG, :].bitcast(I32),
-                in_=w0_scales[:, 4 * q : 4 * q + 4, :].rearrange("g q n -> q g n").bitcast(I32),
-            )
-        for q in range(4):
-            nc.gpsimd.dma_start(
-                out=wsc[32 * q : 32 * q + 4, KG, :].bitcast(I32),
-                in_=a_scales[0, 4 * q : 4 * q + 4, :].bitcast(I32),
-            )
         load_x(1)
         load_x(2)
         load_x(3)
-        load_b(1, 0)
-        load_b(1, 1)
-        nc.sync.dma_start(
-            out=w0[:].bitcast(I32),
-            in_=w0_words.rearrange("g p b -> p g b").bitcast(I32),
-        )
+        for g in range(KG):
+            load_b(1, g)
+            load_w0_scales(2 * g)
+            load_w0_scales(2 * g + 1)
+        nc.sync.dma_start(out=w0[:].bitcast(I32), in_=w0_words.rearrange("g p b -> p g b").bitcast(I32))
+        load_a_scales(0)
+        load_a_scales(1)
         nc.sync.dma_start(out=aw[:].bitcast(I32), in_=a_words[0].bitcast(I32))
-        load_b(2, 0)
-        load_b(2, 1)
-        load_b(3, 0)
-        load_b(3, 1)
+        load_a_scales(2)
+        load_a_scales(3)
+        for m in (2, 3):
+            for g in range(KG):
+                load_b(m, g)
 
         grouped = {}
 
         def interleave(m, g, c0, c1, copy):
-            if (m, g) not in grouped:
-                tile_ = work.tile([P, 4 * R], BF16, name="grouped%d_%d" % (m, g), tag="grouped", bufs=8, align_bytes=64)
-                grouped[(m, g)] = tile_
-            dst = grouped[(m, g)][:].rearrange("p (t c i j) -> p c t i j", t=4, i=2, j=4)
+            if m not in grouped:
+                tile_ = work.tile([P, KG, 4 * R], BF16, name="grouped%d" % m, tag="grouped", bufs=NB, align_bytes=64)
+                grouped[m] = tile_
+            dst = grouped[m][:, g, :].rearrange("p (t c i j) -> p c t i j", t=4, i=2, j=4)
             src = braw[m][:, g, :, :].rearrange("p j (c i t) -> p c t i j", i=2, t=4)
             copy(out=dst[:, c0:c1], in_=src[:, c0:c1])
 
-        def quant_b(m, g):
-            nc.vector.quantize_mx(out=bq[m][:, g, :].bitcast(FP8X4), scales=bs[m][:, g, :], in_=grouped[(m, g)][:])
+        def quant_b(m, g0, g1):
+            nc.vector.quantize_mx(
+                out=bq[m][:, g0:g1, :].rearrange("p g r -> p (g r)").bitcast(FP8X4),
+                scales=bs[m][:, g0:g1, :].rearrange("p g r -> p (g r)"),
+                in_=grouped[m][:, g0:g1, :].rearrange("p g r -> p (g r)"),
+            )
 
         def x_turn(i):
             words = x_sb[:, i, :].bitcast(F32)
@@ -147,24 +157,21 @@ def tile_randlorafullrankbasissum_x2_kernel(
 
         def take_x(i):
             bank = banks[("x", i)]
-            dst = xg[:, :, P * i : P * (i + 1), :].rearrange("p g n t -> p g (n t)").bitcast(F32)
-            dst = dst.rearrange("p g (n u) -> p g n u", u=2)
+            dst = xg[:, i, :, :, :].rearrange("p g n t -> p (g n t)").bitcast(F32)
+            dst = dst.rearrange("p (g n u) -> p g n u", g=KG, u=2)
             nc.scalar.copy(out=dst, in_=bank[:].rearrange("p g u n -> p g n u"))
 
-        def quant_x(i0, i1):
-            for g in range(KG):
-                sl = slice(P * i0, P * i1)
-                nc.vector.quantize_mx(
-                    out=xq[:, g, sl].bitcast(FP8X4),
-                    scales=xs[:, g, sl],
-                    in_=xg[:, g, sl, :].rearrange("p n t -> p (n t)"),
-                )
+        def quant_x(i):
+            nc.vector.quantize_mx(
+                out=xq[:, i, :, :].rearrange("p g n -> p (g n)").bitcast(FP8X4),
+                scales=xs[:, i, :, :].rearrange("p g n -> p (g n)"),
+                in_=xg[:, i, :, :, :].rearrange("p g n t -> p (g n t)"),
+            )
 
         banks = {}
 
         def stage1(m, i):
             bank = bank_h("h%d_%d" % (m, i), [P, 4, P])
-            sl = slice(P * i, P * (i + 1))
             for t in range(4):
                 cols = slice(P * t, P * (t + 1))
                 for g in range(KG):
@@ -172,8 +179,8 @@ def tile_randlorafullrankbasissum_x2_kernel(
                         out=bank[:, t, :],
                         lhsT=bq[m][:, g, cols].bitcast(FP8X4),
                         lhsT_scale=bs[m][:, g, cols],
-                        rhs=xq[:, g, sl].bitcast(FP8X4),
-                        rhs_scale=xs[:, g, sl],
+                        rhs=xq[:, i, g, :].bitcast(FP8X4),
+                        rhs_scale=xs[:, i, g, :],
                         start=(g == 0),
                         stop=(g == KG - 1),
                     )
@@ -187,24 +194,24 @@ def tile_randlorafullrankbasissum_x2_kernel(
                 op=MULT,
             )
 
-        def quant_h(m, half):
-            sl = slice(256 * half, 256 * (half + 1))
+        def quant_h(m):
             nc.vector.quantize_mx(
-                out=hq[m][:, sl].bitcast(FP8X4), scales=hs[m][:, sl], in_=hl[m][:, sl, :].rearrange("p n t -> p (n t)")
+                out=hq[m][:].bitcast(FP8X4), scales=hs[m][:], in_=hl[m][:].rearrange("p n t -> p (n t)")
             )
 
         def base(j):
             bank = bank_u("base%d" % j, [P, TOK])
-            for g in range(KG):
-                nc.tensor.matmul_mx(
-                    out=bank[:],
-                    lhsT=w0[:, g, 256 * j : 256 * (j + 1)].bitcast(FP4X4),
-                    lhsT_scale=wsc[:, g, P * j : P * (j + 1)],
-                    rhs=xq[:, g, :].bitcast(FP8X4),
-                    rhs_scale=xs[:, g, :],
-                    start=(g == 0),
-                    stop=(g == KG - 1),
-                )
+            for i in range(TT):
+                for g in range(KG):
+                    nc.tensor.matmul_mx(
+                        out=bank[:, P * i : P * (i + 1)],
+                        lhsT=w0[:, g, 256 * j : 256 * (j + 1)].bitcast(FP4X4),
+                        lhsT_scale=wsc[:, g, P * j : P * (j + 1)],
+                        rhs=xq[:, i, g, :].bitcast(FP8X4),
+                        rhs_scale=xs[:, i, g, :],
+                        start=(g == 0),
+                        stop=(g == KG - 1),
+                    )
             banks[("base", j)] = bank
 
         def take_base(j):
@@ -237,8 +244,7 @@ def tile_randlorafullrankbasissum_x2_kernel(
         def out_bank(j):
             bank = bank_h("o%d" % j, [P, TT, P])
             parts = [acc[:, j, :]]
-            if not G_ADD:
-                parts = [part[mj][:] for mj in sorted(part) if mj[1] == j] + parts
+            parts = [part[mj][:] for mj in sorted(part) if mj[1] == j and mj not in G_U] + parts
             for i in range(TT):
                 for n, piece in enumerate(parts):
                     nc.tensor.matmul(
@@ -263,22 +269,19 @@ def tile_randlorafullrankbasissum_x2_kernel(
             cols = slice(P * j0, P * j1)
             nc.sync.dma_start(out=out_0[:, cols].rearrange("(i p) f -> p i f", p=P), in_=o32[:, :, cols])
 
-        def round_out(j):
-            h, jj = j // 4, j % 4
-            dst = o16[:].rearrange("p i (h u q e) -> p i h u q e", h=2, u=2, e=2)[:, :, h, :, 32 * jj : 32 * (jj + 1), :]
-            src = o32[:, :, P * j : P * (j + 1)].rearrange("p i (q u e) -> p i u q e", u=2, e=2)
+        def round_out(j, n):
+            cols = slice(P * j, P * (j + n))
             if j in G_CAST:
-                nc.gpsimd.tensor_scalar(out=dst, in0=src, scalar1=1.0, scalar2=-0.0, op0=MULT, op1=ADD)
+                nc.gpsimd.tensor_scalar(out=o16[:, :, cols], in0=o32[:, :, cols], scalar1=1.0, scalar2=-0.0, op0=MULT, op1=ADD)
             else:
-                nc.vector.tensor_copy(out=dst, in_=src)
+                nc.vector.tensor_copy(out=o16[:, :, cols], in_=o32[:, :, cols])
 
         def plane_turn(h, ip):
             bank = bank_h("pt%d_%d" % (h, ip), [P, 2, 2, P])
             for ii in range(2):
                 words = o16[:, 2 * ip + ii, :].bitcast(F32)
                 for u in range(2):
-                    w = 256 * h + 128 * u
-                    nc.tensor.transpose(bank[:, ii, u, :], words[:, w : w + 128], ident[:])
+                    nc.tensor.transpose(bank[:, ii, u, :], words[:, 256 * h + u : 256 * (h + 1) : 2], ident[:])
             banks[("p", h, ip)] = bank
 
         def take_plane(h, ip):
@@ -289,8 +292,8 @@ def tile_randlorafullrankbasissum_x2_kernel(
             copy = nc.vector.tensor_copy if 2 * h + ip in VEC_PL else nc.scalar.copy
             copy(out=dst, in_=bank[:].rearrange("p i u n -> p i n u"))
 
-        def plane_quant(h, ip):
-            sl = slice(256 * ip, 256 * (ip + 1))
+        def plane_quant(h, ip, n):
+            sl = slice(256 * ip, 256 * (ip + n))
             nc.vector.quantize_mx(
                 out=pq[:, h, sl].bitcast(FP8X4), scales=ps[:, h, sl], in_=pg[:, h, sl, :].rearrange("p n t -> p (n t)")
             )
@@ -331,34 +334,39 @@ def tile_randlorafullrankbasissum_x2_kernel(
         for i in range(TT):
             op(("xt", i), "P", 6 * tr, (), lambda i=i: x_turn(i), takes="u", at=at["x"][i])
             op(("tx", i), "S", psr, [("xt", i)], lambda i=i: take_x(i), frees="u")
-            op(("qx", i), "V", 250 + 2 * ov, [("tx", i)], lambda i=i: quant_x(i, i + 1))
+            op(("qx", i), "V", 237 + ov, [("tx", i)], lambda i=i: quant_x(i))
         op("vt", "P", 400, (), turn_vectors, takes="u", at=at["vec"])
         op("tv", "S", 100, ["vt"], take_vectors, frees="u")
         for m in range(NB):
+            deps = {0: [], 1: []}
             for g in range(KG):
-                cut = 16 * VEC_T[m]
-                deps = []
+                cut = VEC_T[m][g]
                 if cut > 0:
-                    deps.append(("iv", m, g))
-                    op(deps[-1], "V", 17.5 * cut + ov, (), lambda m=m, g=g, cut=cut: interleave(m, g, 0, cut, nc.vector.tensor_copy), at=at["b"][2 * m + g])
+                    deps[g].append(("iv", m, g))
+                    op(("iv", m, g), "V", 17.5 * cut + ov, (), lambda m=m, g=g, cut=cut: interleave(m, g, 0, cut, nc.vector.tensor_copy), at=at["b"][2 * m + g])
                 if cut < 64:
-                    deps.append(("is", m, g))
-                    op(deps[-1], "S", 32 * (64 - cut) + ov, (), lambda m=m, g=g, cut=cut: interleave(m, g, cut, 64, nc.scalar.copy), at=at["b"][2 * m + g])
-                op(("qb", m, g), "V", 463 + ov, deps, lambda m=m, g=g: quant_b(m, g))
+                    deps[g].append(("is", m, g))
+                    op(("is", m, g), "S", 32 * (64 - cut) + ov, (), lambda m=m, g=g, cut=cut: interleave(m, g, cut, 64, nc.scalar.copy), at=at["b"][2 * m + g])
+            if m in QB_SPLIT:
+                for g in range(KG):
+                    op(("qb", m, g), "V", 463 + ov, deps[g], lambda m=m, g=g: quant_b(m, g, g + 1))
+                done = [("qb", m, 0), ("qb", m, 1)]
+            else:
+                op(("qb", m), "V", 913 + ov, deps[0] + deps[1], lambda m=m: quant_b(m, 0, KG))
+                done = [("qb", m)]
             for i in range(TT):
-                op(("s1", m, i), "P", 492, [("qb", m, 0), ("qb", m, 1), ("qx", i)], lambda m=m, i=i: stage1(m, i), takes="h")
+                op(("s1", m, i), "P", 492, done + [("qx", i)], lambda m=m, i=i: stage1(m, i), takes="h")
                 op(("tt", m, i), "V", psr, [("s1", m, i), "tv"], lambda m=m, i=i: scale_h(m, i), frees="h")
-            for half in range(2):
-                op(("qh", m, half), "V", 237 + ov, [("tt", m, 2 * half), ("tt", m, 2 * half + 1)], lambda m=m, half=half: quant_h(m, half))
+            op(("qh", m), "V", 463 + ov, [("tt", m, i) for i in range(TT)], lambda m=m: quant_h(m))
         for j in range(NJ):
-            op(("base", j), "P", 440, [("qx", i) for i in range(TT)], lambda j=j: base(j), takes="u", at=at["w"])
+            op(("base", j), "P", 492, [("qx", i) for i in range(TT)], lambda j=j: base(j), takes="u", at=at["w"])
             op(("tb", j), "V" if j in VEC_BASE else "S", psr, [("base", j)], lambda j=j: take_base(j), frees="u")
             last, waits, parts = ("tb", j), [], 1
             for m in range(NB):
-                op(("s2", m, j), "P", 220, [("qh", m, 0), ("qh", m, 1)], lambda m=m, j=j: stage2(m, j), takes="u", at=at["a"])
+                op(("s2", m, j), "P", 220, [("qh", m)], lambda m=m, j=j: stage2(m, j), takes="u", at=at["a"])
                 if (m, j) in S_U:
                     op(("tu", m, j), "S", psr, [("s2", m, j)], lambda m=m, j=j: take_u(m, j), frees="u")
-                    if G_ADD:
+                    if (m, j) in G_U:
                         op(("ga", m, j), "G", T["ga"], [("tu", m, j), last], lambda m=m, j=j: add_u(m, j))
                         last = ("ga", m, j)
                     else:
@@ -369,15 +377,25 @@ def tile_randlorafullrankbasissum_x2_kernel(
                     last = ("tu", m, j)
             op(("o", j), "P", 4 * parts * tr, waits + [last], lambda j=j: out_bank(j), takes="h")
             op(("to", j), "V" if j in VEC_OUT else "S", psr, [("o", j)], lambda j=j: take_out(j), frees="h")
-            op(("rd", j), "G" if j in G_CAST else "V", 600 if j in G_CAST else 215 + ov, [("to", j)], lambda j=j: round_out(j))
         for j in range(0, NJ, 2):
             op(("st", j), "D", 10, [("to", j), ("to", j + 1)], lambda j=j: store(j, j + 2))
+            halves = [(j, 1), (j + 1, 1)] if j in RD_SPLIT else [(j, 2)]
+            for j0, n in halves:
+                deps = [("to", jj) for jj in range(j0, j0 + n)]
+                op(("rd", j0), "G" if j0 in G_CAST else "V", 440 * n + ov if j0 in G_CAST else 215 * n + ov, deps, lambda j0=j0, n=n: round_out(j0, n))
         for h in range(2):
+            rds = [n for n in ops if n[0] == "rd" and 4 * h <= n[1] < 4 * h + 4]
             for ip in range(2):
-                op(("pt", h, ip), "P", 4 * tr, [("rd", j) for j in range(4 * h, 4 * h + 4)], lambda h=h, ip=ip: plane_turn(h, ip), takes="h")
+                op(("pt", h, ip), "P", 6 * tr, rds, lambda h=h, ip=ip: plane_turn(h, ip), takes="h")
                 op(("tp", h, ip), "V" if 2 * h + ip in VEC_PL else "S", psr, [("pt", h, ip)], lambda h=h, ip=ip: take_plane(h, ip), frees="h")
-                op(("pq", h, ip), "V", 237 + ov, [("tp", h, ip)], lambda h=h, ip=ip: plane_quant(h, ip))
-            op(("ps", h), "D", 10, [("pq", h, 0), ("pq", h, 1)], lambda h=h: plane_scales(h))
+            if h in PQ_SPLIT:
+                for ip in range(2):
+                    op(("pq", h, ip), "V", 237 + ov, [("tp", h, ip)], lambda h=h, ip=ip: plane_quant(h, ip, 1))
+                deps = [("pq", h, 0), ("pq", h, 1)]
+            else:
+                op(("pq", h), "V", 463 + ov, [("tp", h, 0), ("tp", h, 1)], lambda h=h: plane_quant(h, 0, 2))
+                deps = [("pq", h)]
+            op(("ps", h), "D", 10, deps, lambda h=h: plane_scales(h))
 
         def order_ops():
             after = {n: [] for n in ops}

@@ -19,25 +19,25 @@ COPY = mybir.ActivationFunctionType.Copy
 
 P = 128
 KG = D // 512
-TT = TOK // P
+NT = TOK // P
 NJ = F // P
 
-S_U = {(1, j) for j in range(NJ)} | {(2, j) for j in (1, 3, 5, 7)}
-VEC_T = ((48, 48), (64, 0), (32, 0), (0, 0))
-QB_SPLIT = (0, 1)
-RD_SPLIT = (6,)
-PQ_SPLIT = (1,)
-G_CAST = (0,)
-G_U = S_U
-VEC_OUT = ()
-VEC_PL = ()
-VEC_BASE = ()
-BANKS = (3, 5)
-TUNE = {}
-DEFAULT_TUNE = dict(
-    ov=100, psr=533, tr=75, ga=950, hop=80, sem=100, raw=150, switch=100, slack=60, bias={"qb": -1000, "qh": -500, "s2": 500, "tb": -500, "to": -4000},
-    at=dict(x=(3400, 4700, 5150, 5600), vec=4000, b=(2950, 4300, 6700, 7700, 10700, 11600, 12500, 13300), w=9200, a=9900),
+GPSIMD_ADDS = {(m, j) for m in (1, 3) for j in (1, 3, 5, 7)} | {(2, 3), (2, 5)}
+TENSOR_ADDS = {(3, 0), (3, 2)}
+SCALAR_U = GPSIMD_ADDS | TENSOR_ADDS
+FIRST_ADD = (3, 3)
+VECTOR_SHARE = ((48, 48), (64, 0), (32, 0), (0, 0))
+BANKS_H, BANKS_U = 3, 5
+
+WEIGHT = dict(
+    turn_x=9, take_x=11, quant_x=7, turn_vectors=8, take_vectors=2, quant_half=11, quant_whole=20, stage1=10,
+    read=11, quant_h=11, base=10, stage2=4, add=19, out=6, round_one=6, round_two=11,
+    turn_plane=9, quant_half_plane=7, quant_plane=11, store=1,
 )
+BIAS = dict(lay_v=40, quant_b=90, quant_h=-40, stage2=-10, take_out=80)
+HOP, LAG, TENSOR_LAG, VECTOR_LAG, SWITCH = 2, 2, 4, 3, 2
+ARRIVE_X, ARRIVE_VECTORS, ARRIVE_W0, ARRIVE_A = (68, 94, 103, 112), 80, 250, 260
+ARRIVE_B = ((59, 86), (134, 154), (174, 192), (280, 300))
 
 
 def tile_randlorafullrankbasissum_x2_kernel(
@@ -46,421 +46,404 @@ def tile_randlorafullrankbasissum_x2_kernel(
     nc = tc.nc
     with ExitStack() as ctx:
         keep = ctx.enter_context(tc.tile_pool(name="keep", bufs=1))
-        work = ctx.enter_context(tc.tile_pool(name="work", bufs=2))
         psum = ctx.enter_context(tc.psum_pool(name="psum", bufs=1))
 
-        def bank_h(name, shape, dtype=F32):
-            return psum.tile(shape, dtype, name=name, tag="bank_h", bufs=BANKS[0])
+        def bank_h(name, shape):
+            return psum.tile(shape, F32, name=name, tag="bank_h", bufs=BANKS_H)
 
         def bank_u(name, shape, dtype=F32):
-            return psum.tile(shape, dtype, name=name, tag="bank_u", bufs=BANKS[1])
+            return psum.tile(shape, dtype, name=name, tag="bank_u", bufs=BANKS_U)
 
-        x_sb = keep.tile([P, TT, D], BF16, name="x_sb", align_bytes=64)
-        xg = keep.tile([P, TT, KG, P, 4], BF16, name="xg", align_bytes=64)
-        xq = keep.tile([P, TT, KG, P], U32, name="xq", align_bytes=64)
-        xs = keep.tile([P, TT, KG, P], U8, name="xs", align_bytes=64)
-        braw = [keep.tile([P, KG, 4, R], BF16, name="braw%d" % m, align_bytes=64) for m in range(NB)]
-        bq = [keep.tile([P, KG, R], U32, name="bq%d" % m, align_bytes=64) for m in range(NB)]
-        bs = [keep.tile([P, KG, R], U8, name="bs%d" % m, align_bytes=64) for m in range(NB)]
-        w0 = keep.tile([P, KG, 2 * F], U8, name="w0", align_bytes=64)
-        aw = keep.tile([P, 2 * F], U8, name="aw", align_bytes=64)
-        wsc = keep.tile([P, KG + 1, F], U8, name="wsc", align_bytes=64)
-        vec = keep.tile([P, R + P], BF16, name="vec", align_bytes=64)
-        ident = keep.tile([P, P], F32, name="ident", align_bytes=64)
-        ident_b = keep.tile([P, P], BF16, name="ident_b", align_bytes=64)
-        lam_t = keep.tile([P, NB, 1, 4], F32, name="lam_t", align_bytes=64)
-        gam_t = keep.tile([P, NB * NJ], F32, name="gam_t", align_bytes=64)
-        acc = keep.tile([P, NJ, TOK], F32, name="acc", align_bytes=64)
-        o32 = keep.tile([P, TT, F], F32, name="o32", align_bytes=64)
-        o16 = keep.tile([P, TT, F], BF16, name="o16", align_bytes=64)
-        pg = keep.tile([P, 2, TOK, 4], BF16, name="pg", align_bytes=64)
-        pq = keep.tile([P, 2, TOK], U32, name="pq", align_bytes=64)
-        ps = keep.tile([P, 2, TOK], U8, name="ps", align_bytes=64)
-        hl = [keep.tile([P, TOK, 4], BF16, name="hl%d" % m, align_bytes=64) for m in range(NB)]
-        hq = [keep.tile([P, TOK], U32, name="hq%d" % m, align_bytes=64) for m in range(NB)]
-        hs = [keep.tile([P, TOK], U8, name="hs%d" % m, align_bytes=64) for m in range(NB)]
-        part = {}
-        for m, j in sorted(S_U):
-            part[(m, j)] = keep.tile([P, TOK], F32, name="part%d_%d" % (m, j), align_bytes=64)
+        def sbuf(name, shape, dtype):
+            return keep.tile(shape, dtype, name=name, align_bytes=64)
 
-        nc.vector.memset(vec[:], 0.0)
+        x_sb = sbuf("x_sb", [P, NT, D], BF16)
+        x_in = sbuf("x_in", [P, NT, KG, P, 4], BF16)
+        x_codes = sbuf("x_codes", [P, NT, KG, P], U32)
+        x_scales = sbuf("x_scales", [P, NT, KG, P], U8)
+        b_sb = [sbuf("b_sb%d" % m, [P, KG, 4, R], BF16) for m in range(NB)]
+        b_in = [sbuf("b_in%d" % m, [P, KG, 4 * R], BF16) for m in range(NB)]
+        b_codes = [sbuf("b_codes%d" % m, [P, KG, R], U32) for m in range(NB)]
+        b_scales = [sbuf("b_scales%d" % m, [P, KG, R], U8) for m in range(NB)]
+        w0_sb = sbuf("w0_sb", [P, KG, 2 * F], U8)
+        a_sb = sbuf("a_sb", [P, 2 * F], U8)
+        w_scales = sbuf("w_scales", [P, KG + 1, F], U8)
+        vectors = sbuf("vectors", [P, R + P], BF16)
+        ident = sbuf("ident", [P, P], F32)
+        ident_b = sbuf("ident_b", [P, P], BF16)
+        lam_t = sbuf("lam_t", [P, NB, 1, 4], F32)
+        gam_t = sbuf("gam_t", [P, NB * NJ], F32)
+        hl = [sbuf("hl%d" % m, [P, TOK, 4], BF16) for m in range(NB)]
+        h_codes = [sbuf("h_codes%d" % m, [P, TOK], U32) for m in range(NB)]
+        h_scales = [sbuf("h_scales%d" % m, [P, TOK], U8) for m in range(NB)]
+        acc = sbuf("acc", [P, NJ, TOK], F32)
+        scaled = {mj: sbuf("scaled%d_%d" % mj, [P, TOK], F32) for mj in sorted(SCALAR_U)}
+        o32 = sbuf("o32", [P, NT, F], F32)
+        o16 = sbuf("o16", [P, NT, F], BF16)
+        p_in = sbuf("p_in", [P, 2, TOK, 4], BF16)
+        p_codes = sbuf("p_codes", [P, 2, TOK], U32)
+        p_scales = sbuf("p_scales", [P, 2, TOK], U8)
+
+        nc.vector.memset(vectors[:], 0.0)
         make_identity(nc, ident[:])
-        nc.gpsimd.memset(wsc[:].rearrange("p a n -> p (a n)").bitcast(I32), 0)
+        nc.gpsimd.memset(w_scales[:].rearrange("p a n -> p (a n)").bitcast(I32), 0)
         nc.scalar.copy(out=ident_b[:], in_=ident[:])
 
         def load_x(i):
             nc.sync.dma_start(out=x_sb[:, i, :], in_=x[P * i : P * (i + 1), :])
 
         def load_b(m, g):
-            nc.sync.dma_start(
-                out=braw[m][:, g, :, :],
-                in_=bases[m, 512 * g : 512 * (g + 1), :].rearrange("(p j) r -> p j r", j=4),
-            )
+            rows = bases[m, 512 * g : 512 * (g + 1), :]
+            nc.sync.dma_start(out=b_sb[m][:, g, :, :], in_=rows.rearrange("(p t) r -> p t r", t=4))
 
         def load_w0_scales(q):
             nc.sync.dma_start(
-                out=wsc[32 * q : 32 * q + 4, 0:KG, :].bitcast(I32),
+                out=w_scales[32 * q : 32 * q + 4, 0:KG, :].bitcast(I32),
                 in_=w0_scales[:, 4 * q : 4 * q + 4, :].rearrange("g q n -> q g n").bitcast(I32),
             )
 
         def load_a_scales(q):
             nc.sync.dma_start(
-                out=wsc[32 * q : 32 * q + 4, KG, :].bitcast(I32), in_=a_scales[0, 4 * q : 4 * q + 4, :].bitcast(I32)
+                out=w_scales[32 * q : 32 * q + 4, KG, :].bitcast(I32),
+                in_=a_scales[0, 4 * q : 4 * q + 4, :].bitcast(I32),
             )
 
         load_b(0, 0)
         load_x(0)
         load_b(0, 1)
-        nc.scalar.dma_start(out=vec[0:NB, 0:R], in_=lam[:, :])
-        nc.scalar.dma_start(out=vec[0 : NB * NJ, R : R + P], in_=gam.rearrange("m (j p) -> (m j) p", p=P))
-        load_x(1)
-        load_x(2)
-        load_x(3)
-        for g in range(KG):
-            load_b(1, g)
-            load_w0_scales(2 * g)
-            load_w0_scales(2 * g + 1)
-        nc.sync.dma_start(out=w0[:].bitcast(I32), in_=w0_words.rearrange("g p b -> p g b").bitcast(I32))
-        load_a_scales(0)
-        load_a_scales(1)
-        nc.sync.dma_start(out=aw[:].bitcast(I32), in_=a_words[0].bitcast(I32))
-        load_a_scales(2)
-        load_a_scales(3)
-        for m in (2, 3):
+        nc.scalar.dma_start(out=vectors[0:NB, 0:R], in_=lam[:, :])
+        nc.scalar.dma_start(out=vectors[0 : NB * NJ, R : R + P], in_=gam.rearrange("m (j p) -> (m j) p", p=P))
+        for i in range(1, NT):
+            load_x(i)
+        for m in (1, 2):
             for g in range(KG):
                 load_b(m, g)
+        nc.sync.dma_start(out=w0_sb[:].bitcast(I32), in_=w0_words.rearrange("g p b -> p g b").bitcast(I32))
+        nc.sync.dma_start(out=a_sb[:].bitcast(I32), in_=a_words[0].bitcast(I32))
+        for q in range(4):
+            load_w0_scales(q)
+        for q in range(4):
+            load_a_scales(q)
+        for g in range(KG):
+            load_b(3, g)
 
-        grouped = {}
+        banks = {}
 
-        def interleave(m, g, c0, c1, copy):
-            if m not in grouped:
-                tile_ = work.tile([P, KG, 4 * R], BF16, name="grouped%d" % m, tag="grouped", bufs=NB, align_bytes=64)
-                grouped[m] = tile_
-            dst = grouped[m][:, g, :].rearrange("p (t c i j) -> p c t i j", t=4, i=2, j=4)
-            src = braw[m][:, g, :, :].rearrange("p j (c i t) -> p c t i j", i=2, t=4)
+        def turn_x(i):
+            words = x_sb[:, i, :].bitcast(F32)
+            banks["x", i] = bank_u("x%d" % i, [P, KG, 2, P])
+            for g in range(KG):
+                for u in range(2):
+                    nc.tensor.transpose(
+                        banks["x", i][:, g, u, :], words[:, 256 * g + u : 256 * (g + 1) : 2], ident[:]
+                    )
+
+        def take_x(i):
+            dst = x_in[:, i, :, :, :].rearrange("p g n t -> p (g n t)").bitcast(F32)
+            nc.scalar.copy(
+                out=dst.rearrange("p (g n u) -> p g n u", g=KG, u=2),
+                in_=banks["x", i][:].rearrange("p g u n -> p g n u"),
+            )
+
+        def quant_x(i):
+            nc.vector.quantize_mx(
+                out=x_codes[:, i, :, :].rearrange("p g n -> p (g n)").bitcast(FP8X4),
+                scales=x_scales[:, i, :, :].rearrange("p g n -> p (g n)"),
+                in_=x_in[:, i, :, :, :].rearrange("p g n t -> p (g n t)"),
+            )
+
+        def turn_vectors():
+            banks["v"] = bank_u("v", [P, 5, P], BF16)
+            for t in range(4):
+                nc.tensor.transpose(banks["v"][:, t, :], vectors[:, t:R:4], ident_b[:])
+            nc.tensor.transpose(banks["v"][:, 4, :], vectors[:, R : R + P], ident_b[:])
+
+        def take_vectors():
+            nc.scalar.copy(
+                out=lam_t[:].rearrange("p m o t -> p m (o t)"),
+                in_=banks["v"][:, 0:4, 0:NB].rearrange("p t m -> p m t"),
+            )
+            nc.scalar.copy(out=gam_t[:], in_=banks["v"][:, 4, 0 : NB * NJ])
+
+        def lay_out_b(m, g, c0, c1, copy):
+            dst = b_in[m][:, g, :].rearrange("p (t c i k) -> p c t i k", t=4, i=2, k=4)
+            src = b_sb[m][:, g, :, :].rearrange("p k (c i t) -> p c t i k", i=2, t=4)
             copy(out=dst[:, c0:c1], in_=src[:, c0:c1])
 
         def quant_b(m, g0, g1):
             nc.vector.quantize_mx(
-                out=bq[m][:, g0:g1, :].rearrange("p g r -> p (g r)").bitcast(FP8X4),
-                scales=bs[m][:, g0:g1, :].rearrange("p g r -> p (g r)"),
-                in_=grouped[m][:, g0:g1, :].rearrange("p g r -> p (g r)"),
+                out=b_codes[m][:, g0:g1, :].rearrange("p g r -> p (g r)").bitcast(FP8X4),
+                scales=b_scales[m][:, g0:g1, :].rearrange("p g r -> p (g r)"),
+                in_=b_in[m][:, g0:g1, :].rearrange("p g r -> p (g r)"),
             )
-
-        def x_turn(i):
-            words = x_sb[:, i, :].bitcast(F32)
-            bank = bank_u("xt%d" % i, [P, KG, 2, P])
-            for g in range(KG):
-                for u in range(2):
-                    nc.tensor.transpose(bank[:, g, u, :], words[:, 256 * g + u : 256 * (g + 1) : 2], ident[:])
-            banks[("x", i)] = bank
-
-        def take_x(i):
-            bank = banks[("x", i)]
-            dst = xg[:, i, :, :, :].rearrange("p g n t -> p (g n t)").bitcast(F32)
-            dst = dst.rearrange("p (g n u) -> p g n u", g=KG, u=2)
-            nc.scalar.copy(out=dst, in_=bank[:].rearrange("p g u n -> p g n u"))
-
-        def quant_x(i):
-            nc.vector.quantize_mx(
-                out=xq[:, i, :, :].rearrange("p g n -> p (g n)").bitcast(FP8X4),
-                scales=xs[:, i, :, :].rearrange("p g n -> p (g n)"),
-                in_=xg[:, i, :, :, :].rearrange("p g n t -> p (g n t)"),
-            )
-
-        banks = {}
 
         def stage1(m, i):
-            bank = bank_h("h%d_%d" % (m, i), [P, 4, P])
+            banks["h", m, i] = bank_h("h%d_%d" % (m, i), [P, 4, P])
             for t in range(4):
                 cols = slice(P * t, P * (t + 1))
                 for g in range(KG):
                     nc.tensor.matmul_mx(
-                        out=bank[:, t, :],
-                        lhsT=bq[m][:, g, cols].bitcast(FP8X4),
-                        lhsT_scale=bs[m][:, g, cols],
-                        rhs=xq[:, i, g, :].bitcast(FP8X4),
-                        rhs_scale=xs[:, i, g, :],
+                        out=banks["h", m, i][:, t, :],
+                        lhsT=b_codes[m][:, g, cols].bitcast(FP8X4),
+                        lhsT_scale=b_scales[m][:, g, cols],
+                        rhs=x_codes[:, i, g, :].bitcast(FP8X4),
+                        rhs_scale=x_scales[:, i, g, :],
                         start=(g == 0),
                         stop=(g == KG - 1),
                     )
-            banks[(m, i)] = bank
 
         def scale_h(m, i):
             nc.vector.tensor_tensor(
                 out=hl[m][:, P * i : P * (i + 1), :],
-                in0=banks[(m, i)][:].rearrange("p t n -> p n t"),
+                in0=banks["h", m, i][:].rearrange("p t n -> p n t"),
                 in1=lam_t[:, m, :, :].to_broadcast([P, P, 4]),
                 op=MULT,
             )
 
         def quant_h(m):
             nc.vector.quantize_mx(
-                out=hq[m][:].bitcast(FP8X4), scales=hs[m][:], in_=hl[m][:].rearrange("p n t -> p (n t)")
+                out=h_codes[m][:].bitcast(FP8X4),
+                scales=h_scales[m][:],
+                in_=hl[m][:].rearrange("p n t -> p (n t)"),
             )
 
         def base(j):
-            bank = bank_u("base%d" % j, [P, TOK])
-            for i in range(TT):
+            banks["base", j] = bank_u("base%d" % j, [P, TOK])
+            for i in range(NT):
                 for g in range(KG):
                     nc.tensor.matmul_mx(
-                        out=bank[:, P * i : P * (i + 1)],
-                        lhsT=w0[:, g, 256 * j : 256 * (j + 1)].bitcast(FP4X4),
-                        lhsT_scale=wsc[:, g, P * j : P * (j + 1)],
-                        rhs=xq[:, i, g, :].bitcast(FP8X4),
-                        rhs_scale=xs[:, i, g, :],
+                        out=banks["base", j][:, P * i : P * (i + 1)],
+                        lhsT=w0_sb[:, g, 256 * j : 256 * (j + 1)].bitcast(FP4X4),
+                        lhsT_scale=w_scales[:, g, P * j : P * (j + 1)],
+                        rhs=x_codes[:, i, g, :].bitcast(FP8X4),
+                        rhs_scale=x_scales[:, i, g, :],
                         start=(g == 0),
                         stop=(g == KG - 1),
                     )
-            banks[("base", j)] = bank
 
         def take_base(j):
-            copy = nc.vector.tensor_copy if j in VEC_BASE else nc.scalar.copy
-            copy(out=acc[:, j, :], in_=banks[("base", j)][:])
+            nc.scalar.copy(out=acc[:, j, :], in_=banks["base", j][:])
 
         def stage2(m, j):
-            bank = bank_u("u%d_%d" % (m, j), [P, TOK])
+            banks["u", m, j] = bank_u("u%d_%d" % (m, j), [P, TOK])
             nc.tensor.matmul_mx(
-                out=bank[:],
-                lhsT=aw[:, 256 * j : 256 * (j + 1)].bitcast(FP4X4),
-                lhsT_scale=wsc[:, KG, P * j : P * (j + 1)],
-                rhs=hq[m][:].bitcast(FP8X4),
-                rhs_scale=hs[m][:],
+                out=banks["u", m, j][:],
+                lhsT=a_sb[:, 256 * j : 256 * (j + 1)].bitcast(FP4X4),
+                lhsT_scale=w_scales[:, KG, P * j : P * (j + 1)],
+                rhs=h_codes[m][:].bitcast(FP8X4),
+                rhs_scale=h_scales[m][:],
                 start=True,
                 stop=True,
             )
-            banks[("u", m, j)] = bank
 
         def take_u(m, j):
-            bank = banks[("u", m, j)]
-            col = gam_t[:, NJ * m + j : NJ * m + j + 1]
-            if (m, j) in S_U:
-                nc.scalar.activation(out=part[(m, j)][:], in_=bank[:], func=COPY, scale=col)
+            gam_col = gam_t[:, NJ * m + j : NJ * m + j + 1]
+            if (m, j) in SCALAR_U:
+                nc.scalar.activation(out=scaled[m, j][:], in_=banks["u", m, j][:], func=COPY, scale=gam_col)
             else:
                 nc.vector.scalar_tensor_tensor(
-                    out=acc[:, j, :], in0=bank[:], scalar=col, in1=acc[:, j, :], op0=MULT, op1=ADD
+                    out=acc[:, j, :], in0=banks["u", m, j][:], scalar=gam_col, in1=acc[:, j, :], op0=MULT, op1=ADD
                 )
 
-        def out_bank(j):
-            bank = bank_h("o%d" % j, [P, TT, P])
-            parts = [acc[:, j, :]]
-            parts = [part[mj][:] for mj in sorted(part) if mj[1] == j and mj not in G_U] + parts
-            for i in range(TT):
-                for n, piece in enumerate(parts):
+        def add_u(m, j):
+            nc.gpsimd.tensor_tensor(out=acc[:, j, :], in0=acc[:, j, :], in1=scaled[m, j][:], op=ADD)
+
+        def turn_out(j):
+            banks["o", j] = bank_h("o%d" % j, [P, NT, P])
+            parts = [scaled[mj][:] for mj in sorted(TENSOR_ADDS) if mj[1] == j] + [acc[:, j, :]]
+            for i in range(NT):
+                for n, part in enumerate(parts):
                     nc.tensor.matmul(
-                        bank[:, i, :],
-                        lhsT=piece[:, P * i : P * (i + 1)],
+                        banks["o", j][:, i, :],
+                        lhsT=part[:, P * i : P * (i + 1)],
                         rhs=ident[:],
                         start=(n == 0),
                         stop=(n == len(parts) - 1),
                         is_transpose=True,
                     )
-            banks[("o", j)] = bank
-
-        def add_u(m, j):
-            nc.gpsimd.tensor_tensor(out=acc[:, j, :], in0=acc[:, j, :], in1=part[(m, j)][:], op=ADD)
 
         def take_out(j):
-            cols = slice(P * j, P * (j + 1))
-            copy = nc.vector.tensor_copy if j in VEC_OUT else nc.scalar.copy
-            copy(out=o32[:, :, cols], in_=banks[("o", j)][:])
+            nc.scalar.copy(out=o32[:, :, P * j : P * (j + 1)], in_=banks["o", j][:])
 
         def store(j0, j1):
             cols = slice(P * j0, P * j1)
             nc.sync.dma_start(out=out_0[:, cols].rearrange("(i p) f -> p i f", p=P), in_=o32[:, :, cols])
 
-        def round_out(j, n):
-            cols = slice(P * j, P * (j + n))
-            if j in G_CAST:
-                nc.gpsimd.tensor_scalar(out=o16[:, :, cols], in0=o32[:, :, cols], scalar1=1.0, scalar2=-0.0, op0=MULT, op1=ADD)
-            else:
-                nc.vector.tensor_copy(out=o16[:, :, cols], in_=o32[:, :, cols])
+        def round_out(j0, j1):
+            cols = slice(P * j0, P * j1)
+            nc.vector.tensor_copy(out=o16[:, :, cols], in_=o32[:, :, cols])
 
-        def plane_turn(h, ip):
-            bank = bank_h("pt%d_%d" % (h, ip), [P, 2, 2, P])
+        def turn_plane(h, half):
+            banks["p", h, half] = bank_h("p%d_%d" % (h, half), [P, 2, 2, P])
             for ii in range(2):
-                words = o16[:, 2 * ip + ii, :].bitcast(F32)
+                words = o16[:, 2 * half + ii, :].bitcast(F32)
                 for u in range(2):
-                    nc.tensor.transpose(bank[:, ii, u, :], words[:, 256 * h + u : 256 * (h + 1) : 2], ident[:])
-            banks[("p", h, ip)] = bank
+                    nc.tensor.transpose(
+                        banks["p", h, half][:, ii, u, :], words[:, 256 * h + u : 256 * (h + 1) : 2], ident[:]
+                    )
 
-        def take_plane(h, ip):
-            bank = banks[("p", h, ip)]
-            sl = slice(256 * ip, 256 * (ip + 1))
-            dst = pg[:, h, sl, :].rearrange("p n t -> p (n t)").bitcast(F32)
-            dst = dst.rearrange("p (i n u) -> p i n u", i=2, u=2)
-            copy = nc.vector.tensor_copy if 2 * h + ip in VEC_PL else nc.scalar.copy
-            copy(out=dst, in_=bank[:].rearrange("p i u n -> p i n u"))
+        def take_plane(h, half):
+            dst = p_in[:, h, 256 * half : 256 * (half + 1), :].rearrange("p n t -> p (n t)").bitcast(F32)
+            nc.scalar.copy(
+                out=dst.rearrange("p (i n u) -> p i n u", i=2, u=2),
+                in_=banks["p", h, half][:].rearrange("p i u n -> p i n u"),
+            )
 
-        def plane_quant(h, ip, n):
-            sl = slice(256 * ip, 256 * (ip + n))
+        def quant_plane(h, n0, n1):
             nc.vector.quantize_mx(
-                out=pq[:, h, sl].bitcast(FP8X4), scales=ps[:, h, sl], in_=pg[:, h, sl, :].rearrange("p n t -> p (n t)")
+                out=p_codes[:, h, n0:n1].bitcast(FP8X4),
+                scales=p_scales[:, h, n0:n1],
+                in_=p_in[:, h, n0:n1, :].rearrange("p n t -> p (n t)"),
             )
-            nc.sync.dma_start(
-                out=out_1[h].rearrange("p n t -> p (n t)").bitcast(I32)[:, sl], in_=pq[:, h, sl].bitcast(I32)
-            )
+            words = out_1[h].rearrange("p n t -> p (n t)").bitcast(I32)
+            nc.sync.dma_start(out=words[:, n0:n1], in_=p_codes[:, h, n0:n1].bitcast(I32))
 
-        def plane_scales(h):
+        def store_scales(h):
             for q in range(4):
-                eng = nc.sync if q % 2 == 0 else nc.scalar
-                eng.dma_start(
-                    out=out_2[h, 4 * q : 4 * q + 4, :].bitcast(I32), in_=ps[32 * q : 32 * q + 4, h, :].bitcast(I32)
+                queue = nc.sync if q % 2 == 0 else nc.scalar
+                queue.dma_start(
+                    out=out_2[h, 4 * q : 4 * q + 4, :].bitcast(I32),
+                    in_=p_scales[32 * q : 32 * q + 4, h, :].bitcast(I32),
                 )
 
-        def turn_vectors():
-            vbank = bank_u("vbank", [P, 5, P], BF16)
-            for t in range(4):
-                nc.tensor.transpose(vbank[:, t, :], vec[:, t:R:4], ident_b[:])
-            nc.tensor.transpose(vbank[:, 4, :], vec[:, R : R + P], ident_b[:])
-            banks["v"] = vbank
+        steps = {}
 
-        def take_vectors():
-            vbank = banks["v"]
-            nc.scalar.copy(
-                out=lam_t[:].rearrange("p m o t -> p m (o t)"), in_=vbank[:, 0:4, 0:NB].rearrange("p t m -> p m t")
-            )
-            nc.scalar.copy(out=gam_t[:], in_=vbank[:, 4, 0 : NB * NJ])
+        def step(name, engine, weight, after, fn, args, takes=None, frees=None, at=0):
+            steps[name] = (engine, weight, after, takes, frees, at, fn, args)
 
-        ops = {}
-
-        def op(name, engine, weight, deps, fn, takes=None, frees=None, at=0):
-            ops[name] = (engine, weight, tuple(deps), fn, takes, frees, at)
-
-        T = dict(DEFAULT_TUNE)
-        T.update(TUNE)
-        ov, psr, tr = T["ov"], T["psr"], T["tr"]
-        at = T["at"]
-        for i in range(TT):
-            op(("xt", i), "P", 6 * tr, (), lambda i=i: x_turn(i), takes="u", at=at["x"][i])
-            op(("tx", i), "S", psr, [("xt", i)], lambda i=i: take_x(i), frees="u")
-            op(("qx", i), "V", 237 + ov, [("tx", i)], lambda i=i: quant_x(i))
-        op("vt", "P", 400, (), turn_vectors, takes="u", at=at["vec"])
-        op("tv", "S", 100, ["vt"], take_vectors, frees="u")
+        read = WEIGHT["read"]
+        for i in range(NT):
+            step(("turn_x", i), "T", WEIGHT["turn_x"], [], turn_x, (i,), takes="u", at=ARRIVE_X[i])
+            step(("take_x", i), "S", WEIGHT["take_x"], [("turn_x", i)], take_x, (i,), frees="u")
+            step(("quant_x", i), "V", WEIGHT["quant_x"], [("take_x", i)], quant_x, (i,))
+        step(("turn_vectors",), "T", WEIGHT["turn_vectors"], [], turn_vectors, (), takes="u", at=ARRIVE_VECTORS)
+        step(("take_vectors",), "S", WEIGHT["take_vectors"], [("turn_vectors",)], take_vectors, (), frees="u")
         for m in range(NB):
-            deps = {0: [], 1: []}
+            laid = []
             for g in range(KG):
-                cut = VEC_T[m][g]
+                cut = VECTOR_SHARE[m][g]
                 if cut > 0:
-                    deps[g].append(("iv", m, g))
-                    op(("iv", m, g), "V", 17.5 * cut + ov, (), lambda m=m, g=g, cut=cut: interleave(m, g, 0, cut, nc.vector.tensor_copy), at=at["b"][2 * m + g])
+                    args = (m, g, 0, cut, nc.vector.tensor_copy)
+                    step(("lay_v", m, g), "V", (35 * cut) // 100 + 2, [], lay_out_b, args, at=ARRIVE_B[m][g])
+                    laid.append(("lay_v", m, g))
                 if cut < 64:
-                    deps[g].append(("is", m, g))
-                    op(("is", m, g), "S", 32 * (64 - cut) + ov, (), lambda m=m, g=g, cut=cut: interleave(m, g, cut, 64, nc.scalar.copy), at=at["b"][2 * m + g])
-            if m in QB_SPLIT:
-                for g in range(KG):
-                    op(("qb", m, g), "V", 463 + ov, deps[g], lambda m=m, g=g: quant_b(m, g, g + 1))
-                done = [("qb", m, 0), ("qb", m, 1)]
-            else:
-                op(("qb", m), "V", 913 + ov, deps[0] + deps[1], lambda m=m: quant_b(m, 0, KG))
-                done = [("qb", m)]
-            for i in range(TT):
-                op(("s1", m, i), "P", 492, done + [("qx", i)], lambda m=m, i=i: stage1(m, i), takes="h")
-                op(("tt", m, i), "V", psr, [("s1", m, i), "tv"], lambda m=m, i=i: scale_h(m, i), frees="h")
-            op(("qh", m), "V", 463 + ov, [("tt", m, i) for i in range(TT)], lambda m=m: quant_h(m))
+                    args = (m, g, cut, 64, nc.scalar.copy)
+                    step(("lay_s", m, g), "S", (64 * (64 - cut)) // 100 + 2, [], lay_out_b, args, at=ARRIVE_B[m][g])
+                    laid.append(("lay_s", m, g))
+                if m == 0:
+                    step(("quant_b", m, g), "V", WEIGHT["quant_half"], laid, quant_b, (m, g, g + 1))
+                    laid = []
+            quantised = [("quant_b", 0, 0), ("quant_b", 0, 1)]
+            if m > 0:
+                step(("quant_b", m), "V", WEIGHT["quant_whole"], laid, quant_b, (m, 0, KG))
+                quantised = [("quant_b", m)]
+            for i in range(NT):
+                step(("stage1", m, i), "T", WEIGHT["stage1"], quantised + [("quant_x", i)], stage1, (m, i), takes="h")
+                after = [("stage1", m, i), ("take_vectors",)]
+                step(("scale", m, i), "V", read, after, scale_h, (m, i), frees="h")
+            step(("quant_h", m), "V", WEIGHT["quant_h"], [("scale", m, i) for i in range(NT)], quant_h, (m,))
         for j in range(NJ):
-            op(("base", j), "P", 492, [("qx", i) for i in range(TT)], lambda j=j: base(j), takes="u", at=at["w"])
-            op(("tb", j), "V" if j in VEC_BASE else "S", psr, [("base", j)], lambda j=j: take_base(j), frees="u")
-            last, waits, parts = ("tb", j), [], 1
+            after = [("quant_x", i) for i in range(NT)]
+            step(("base", j), "T", WEIGHT["base"], after, base, (j,), takes="u", at=ARRIVE_W0)
+            step(("take_base", j), "S", read, [("base", j)], take_base, (j,), frees="u")
             for m in range(NB):
-                op(("s2", m, j), "P", 220, [("qh", m)], lambda m=m, j=j: stage2(m, j), takes="u", at=at["a"])
-                if (m, j) in S_U:
-                    op(("tu", m, j), "S", psr, [("s2", m, j)], lambda m=m, j=j: take_u(m, j), frees="u")
-                    if (m, j) in G_U:
-                        op(("ga", m, j), "G", T["ga"], [("tu", m, j), last], lambda m=m, j=j: add_u(m, j))
-                        last = ("ga", m, j)
-                    else:
-                        waits.append(("tu", m, j))
-                        parts += 1
-                else:
-                    op(("tu", m, j), "V", psr, [("s2", m, j), last], lambda m=m, j=j: take_u(m, j), frees="u")
-                    last = ("tu", m, j)
-            op(("o", j), "P", 4 * parts * tr, waits + [last], lambda j=j: out_bank(j), takes="h")
-            op(("to", j), "V" if j in VEC_OUT else "S", psr, [("o", j)], lambda j=j: take_out(j), frees="h")
+                step(("stage2", m, j), "T", WEIGHT["stage2"], [("quant_h", m)], stage2, (m, j), takes="u", at=ARRIVE_A)
+            last = ("take_base", j)
+            for m in (3, 0, 1, 2) if j == FIRST_ADD[1] else range(NB):
+                if (m, j) in SCALAR_U:
+                    step(("take_u", m, j), "S", read, [("stage2", m, j)], take_u, (m, j), frees="u")
+                if (m, j) in GPSIMD_ADDS:
+                    after = [("take_u", m, j), last] + ([("add",) + FIRST_ADD] if (m, j) != FIRST_ADD else [])
+                    step(("add", m, j), "G", WEIGHT["add"], after, add_u, (m, j))
+                    last = ("add", m, j)
+                elif (m, j) not in SCALAR_U:
+                    step(("take_u", m, j), "V", read, [("stage2", m, j), last], take_u, (m, j), frees="u")
+                    last = ("take_u", m, j)
+            apart = [("take_u",) + mj for mj in sorted(TENSOR_ADDS) if mj[1] == j]
+            weight = WEIGHT["out"] * (1 + len(apart))
+            step(("turn_out", j), "T", weight, apart + [last], turn_out, (j,), takes="h")
+            step(("take_out", j), "S", read, [("turn_out", j)], take_out, (j,), frees="h")
         for j in range(0, NJ, 2):
-            op(("st", j), "D", 10, [("to", j), ("to", j + 1)], lambda j=j: store(j, j + 2))
-            halves = [(j, 1), (j + 1, 1)] if j in RD_SPLIT else [(j, 2)]
-            for j0, n in halves:
-                deps = [("to", jj) for jj in range(j0, j0 + n)]
-                op(("rd", j0), "G" if j0 in G_CAST else "V", 440 * n + ov if j0 in G_CAST else 215 * n + ov, deps, lambda j0=j0, n=n: round_out(j0, n))
-        for h in range(2):
-            rds = [n for n in ops if n[0] == "rd" and 4 * h <= n[1] < 4 * h + 4]
-            for ip in range(2):
-                op(("pt", h, ip), "P", 6 * tr, rds, lambda h=h, ip=ip: plane_turn(h, ip), takes="h")
-                op(("tp", h, ip), "V" if 2 * h + ip in VEC_PL else "S", psr, [("pt", h, ip)], lambda h=h, ip=ip: take_plane(h, ip), frees="h")
-            if h in PQ_SPLIT:
-                for ip in range(2):
-                    op(("pq", h, ip), "V", 237 + ov, [("tp", h, ip)], lambda h=h, ip=ip: plane_quant(h, ip, 1))
-                deps = [("pq", h, 0), ("pq", h, 1)]
+            pair = [("take_out", j), ("take_out", j + 1)]
+            step(("store", j), "D", WEIGHT["store"], pair, store, (j, j + 2))
+            if j < NJ // 2:
+                step(("round", j), "V", WEIGHT["round_two"], pair, round_out, (j, j + 2))
             else:
-                op(("pq", h), "V", 463 + ov, [("tp", h, 0), ("tp", h, 1)], lambda h=h: plane_quant(h, 0, 2))
-                deps = [("pq", h)]
-            op(("ps", h), "D", 10, deps, lambda h=h: plane_scales(h))
+                for jj in (j, j + 1):
+                    step(("round", jj), "V", WEIGHT["round_one"], [("take_out", jj)], round_out, (jj, jj + 1))
+        for h in range(2):
+            rounded = [n for n in steps if n[0] == "round" and n[1] // 4 == h]
+            for half in range(2):
+                step(("turn_plane", h, half), "T", WEIGHT["turn_plane"], rounded, turn_plane, (h, half), takes="h")
+                step(("take_plane", h, half), "S", read, [("turn_plane", h, half)], take_plane, (h, half), frees="h")
+            if h == 0:
+                taken = [("take_plane", 0, 0), ("take_plane", 0, 1)]
+                step(("quant_plane", 0), "V", WEIGHT["quant_plane"], taken, quant_plane, (0, 0, TOK))
+            else:
+                for half in range(2):
+                    args = (1, 256 * half, 256 * (half + 1))
+                    after = [("take_plane", 1, half)]
+                    step(("quant_plane", 1, half), "V", WEIGHT["quant_half_plane"], after, quant_plane, args)
+            done = [n for n in steps if n[0] == "quant_plane" and n[1] == h]
+            step(("store_scales", h), "D", WEIGHT["store"], done, store_scales, (h,))
 
-        def order_ops():
-            after = {n: [] for n in ops}
-            for n in ops:
-                for dep in ops[n][2]:
-                    after[dep].append(n)
+        def list_order():
+            followers = {n: [] for n in steps}
+            for n in steps:
+                for before in steps[n][2]:
+                    followers[before].append(n)
             way = {}
-            for n in reversed(list(ops)):
+            for n in steps:
                 stack = [n]
                 while stack:
-                    top = stack[-1]
-                    todo = [a for a in after[top] if a not in way]
-                    if todo:
-                        stack.extend(todo)
+                    open_followers = [f for f in followers[stack[-1]] if f not in way]
+                    if open_followers:
+                        stack.extend(open_followers)
                     else:
-                        way[stack.pop()] = ops[top][1] + T["hop"] + max([way[a] for a in after[top]] + [0])
-            for n in way:
-                kind = n[0] if isinstance(n, tuple) else n
-                way[n] += T["bias"].get(kind, 0)
-            free = {"h": [0] * BANKS[0], "u": [0] * BANKS[1]}
-            clock = {"P": 0, "V": 0, "S": 0, "G": 0, "D": 0}
-            ready = {n: ops[n][6] for n in ops}
-            left = {n: len(ops[n][2]) for n in ops}
-            open_ops = [n for n in ops if left[n] == 0]
-            order, kind_before = [], None
-            while open_ops:
-                best = None
+                        top = stack.pop()
+                        way[top] = steps[top][1] + HOP + max([way[f] for f in followers[top]] + [0])
+            clock = {e: 0 for e in "TVSGD"}
+            free = {"h": [0] * BANKS_H, "u": [0] * BANKS_U}
+            ready = {n: steps[n][5] for n in steps}
+            waits = {n: len(steps[n][2]) for n in steps}
+            startable = [n for n in steps if waits[n] == 0]
+            order, turned_before = [], None
+            while startable:
+                choice = None
                 for e in clock:
                     starts = []
-                    for n in open_ops:
-                        if ops[n][0] == e and (ops[n][4] is None or free[ops[n][4]]):
-                            t = max(clock[e], ready[n])
-                            if ops[n][4]:
-                                t = max(t, min(free[ops[n][4]]))
-                            starts.append((t, n))
+                    for n in startable:
+                        takes = steps[n][3]
+                        if steps[n][0] == e and (takes is None or free[takes]):
+                            starts.append((max(clock[e], ready[n], min(free[takes]) if takes else 0), n))
                     if starts:
-                        soon = min([t for t, n in starts]) + T["slack"]
-                        t, n = max([(way[n], t, str(n), n) for t, n in starts if t <= soon])[1::2]
-                        if best is None or t < best[0]:
-                            best = (t, n)
-                t, n = best
-                e, weight, deps, fn, takes, frees, arrival = ops[n]
+                        soonest = min([t for t, n in starts])
+                        rank = max([(way[n] + BIAS.get(n[0], 0), str(n), n) for t, n in starts if t == soonest])
+                        if choice is None or soonest < choice[0]:
+                            choice = (soonest, rank[2])
+                t, n = choice
+                engine, weight, after, takes, frees = steps[n][:5]
                 if takes:
                     free[takes].remove(min(free[takes]))
-                if e == "P":
-                    k = n[0] in ("xt", "o", "pt") or n == "vt"
-                    if kind_before is not None and k != kind_before:
-                        t += T["switch"]
-                    kind_before = k
-                end = t + weight
-                clock[e] = end
+                if engine == "T":
+                    turned = n[0].startswith("turn")
+                    t += SWITCH if turned_before not in (None, turned) else 0
+                    turned_before = turned
+                clock[engine] = t + weight
                 if frees:
-                    free[frees].append(end + T["sem"])
-                open_ops.remove(n)
+                    free[frees].append(t + weight + LAG)
+                startable.remove(n)
                 order.append(n)
-                for a in after[n]:
-                    lag = T["sem"] + (100 if e == "P" else 0)
-                    if ops[a][0] == e:
-                        lag = T["raw"] if e == "V" else 0
-                    ready[a] = max(ready[a], end + lag)
-                    left[a] -= 1
-                    if left[a] == 0:
-                        open_ops.append(a)
+                for f in followers[n]:
+                    lag = TENSOR_LAG if engine == "T" else LAG
+                    if steps[f][0] == engine:
+                        lag = VECTOR_LAG if engine == "V" else 0
+                    ready[f] = max(ready[f], t + weight + lag)
+                    waits[f] -= 1
+                    if waits[f] == 0:
+                        startable.append(f)
             return order
 
         with tc.manual_schedule():
-            for n in order_ops():
-                ops[n][3]()
+            for n in list_order():
+                steps[n][6](*steps[n][7])

from contextlib import ExitStack

import concourse.mybir as mybir
from concourse.masks import make_identity

TOK, D, NB, R, F = 512, 1024, 4, 512, 1024
FLOPS = 2 * TOK * D * R * NB + 2 * TOK * R * F * NB + 2 * TOK * D * F

F32 = mybir.dt.float32
BF16 = mybir.dt.bfloat16
U32 = mybir.dt.uint32
I32 = mybir.dt.int32
U8 = mybir.dt.uint8
FP8X4 = mybir.dt.float8_e4m3fn_x4
FP4X4 = mybir.dt.float4_e2m1fn_x4
MULT = mybir.AluOpType.mult
ADD = mybir.AluOpType.add
COPY = mybir.ActivationFunctionType.Copy

P = 128
KG = D // 512
NT = TOK // P
NJ = F // P

GPSIMD_ADDS = {(m, j) for m in (1, 3) for j in (1, 3, 5, 7)} | {(2, 3), (2, 5)}
TENSOR_ADDS = {(3, 0), (3, 2)}
SCALAR_U = GPSIMD_ADDS | TENSOR_ADDS
FIRST_ADD = (3, 3)
VECTOR_SHARE = ((48, 48), (64, 0), (32, 0), (0, 0))
BANKS_H, BANKS_U = 3, 5

WEIGHT = dict(
    turn_x=9, take_x=11, quant_x=7, turn_vectors=8, take_vectors=2, quant_half=11, quant_whole=20, stage1=10,
    read=11, quant_h=11, base=10, stage2=4, add=19, out=6, round_one=6, round_two=11,
    turn_plane=9, quant_half_plane=7, quant_plane=11, store=1,
)
BIAS = dict(lay_v=40, quant_b=90, quant_h=-40, stage2=-10, take_out=80)
HOP, LAG, TENSOR_LAG, VECTOR_LAG, SWITCH = 2, 2, 4, 3, 2
ARRIVE_X, ARRIVE_VECTORS, ARRIVE_W0, ARRIVE_A = (68, 94, 103, 112), 80, 250, 260
ARRIVE_B = ((59, 86), (134, 154), (174, 192), (280, 300))


def tile_randlorafullrankbasissum_x2_kernel(
    tc, x, w0_words, w0_scales, bases, lam, a_words, a_scales, gam, out_0, out_1, out_2
):
    nc = tc.nc
    with ExitStack() as ctx:
        keep = ctx.enter_context(tc.tile_pool(name="keep", bufs=1))
        psum = ctx.enter_context(tc.psum_pool(name="psum", bufs=1))

        def bank_h(name, shape):
            return psum.tile(shape, F32, name=name, tag="bank_h", bufs=BANKS_H)

        def bank_u(name, shape, dtype=F32):
            return psum.tile(shape, dtype, name=name, tag="bank_u", bufs=BANKS_U)

        def sbuf(name, shape, dtype):
            return keep.tile(shape, dtype, name=name, align_bytes=64)

        x_sb = sbuf("x_sb", [P, NT, D], BF16)
        x_in = sbuf("x_in", [P, NT, KG, P, 4], BF16)
        x_codes = sbuf("x_codes", [P, NT, KG, P], U32)
        x_scales = sbuf("x_scales", [P, NT, KG, P], U8)
        b_sb = [sbuf("b_sb%d" % m, [P, KG, 4, R], BF16) for m in range(NB)]
        b_in = [sbuf("b_in%d" % m, [P, KG, 4 * R], BF16) for m in range(NB)]
        b_codes = [sbuf("b_codes%d" % m, [P, KG, R], U32) for m in range(NB)]
        b_scales = [sbuf("b_scales%d" % m, [P, KG, R], U8) for m in range(NB)]
        w0_sb = sbuf("w0_sb", [P, KG, 2 * F], U8)
        a_sb = sbuf("a_sb", [P, 2 * F], U8)
        w_scales = sbuf("w_scales", [P, KG + 1, F], U8)
        vectors = sbuf("vectors", [P, R + P], BF16)
        ident = sbuf("ident", [P, P], F32)
        ident_b = sbuf("ident_b", [P, P], BF16)
        lam_t = sbuf("lam_t", [P, NB, 1, 4], F32)
        gam_t = sbuf("gam_t", [P, NB * NJ], F32)
        hl = [sbuf("hl%d" % m, [P, TOK, 4], BF16) for m in range(NB)]
        h_codes = [sbuf("h_codes%d" % m, [P, TOK], U32) for m in range(NB)]
        h_scales = [sbuf("h_scales%d" % m, [P, TOK], U8) for m in range(NB)]
        acc = sbuf("acc", [P, NJ, TOK], F32)
        scaled = {mj: sbuf("scaled%d_%d" % mj, [P, TOK], F32) for mj in sorted(SCALAR_U)}
        o32 = sbuf("o32", [P, NT, F], F32)
        o16 = sbuf("o16", [P, NT, F], BF16)
        p_in = sbuf("p_in", [P, 2, TOK, 4], BF16)
        p_codes = sbuf("p_codes", [P, 2, TOK], U32)
        p_scales = sbuf("p_scales", [P, 2, TOK], U8)

        nc.vector.memset(vectors[:], 0.0)
        make_identity(nc, ident[:])
        nc.gpsimd.memset(w_scales[:].rearrange("p a n -> p (a n)").bitcast(I32), 0)
        nc.scalar.copy(out=ident_b[:], in_=ident[:])

        def load_x(i):
            nc.sync.dma_start(out=x_sb[:, i, :], in_=x[P * i : P * (i + 1), :])

        def load_b(m, g):
            rows = bases[m, 512 * g : 512 * (g + 1), :]
            nc.sync.dma_start(out=b_sb[m][:, g, :, :], in_=rows.rearrange("(p t) r -> p t r", t=4))

        def load_w0_scales(q):
            nc.sync.dma_start(
                out=w_scales[32 * q : 32 * q + 4, 0:KG, :].bitcast(I32),
                in_=w0_scales[:, 4 * q : 4 * q + 4, :].rearrange("g q n -> q g n").bitcast(I32),
            )

        def load_a_scales(q):
            nc.sync.dma_start(
                out=w_scales[32 * q : 32 * q + 4, KG, :].bitcast(I32),
                in_=a_scales[0, 4 * q : 4 * q + 4, :].bitcast(I32),
            )

        load_b(0, 0)
        load_x(0)
        load_b(0, 1)
        nc.scalar.dma_start(out=vectors[0:NB, 0:R], in_=lam[:, :])
        nc.scalar.dma_start(out=vectors[0 : NB * NJ, R : R + P], in_=gam.rearrange("m (j p) -> (m j) p", p=P))
        for i in range(1, NT):
            load_x(i)
        for m in (1, 2):
            for g in range(KG):
                load_b(m, g)
        nc.sync.dma_start(out=w0_sb[:].bitcast(I32), in_=w0_words.rearrange("g p b -> p g b").bitcast(I32))
        nc.sync.dma_start(out=a_sb[:].bitcast(I32), in_=a_words[0].bitcast(I32))
        for q in range(4):
            load_w0_scales(q)
        for q in range(4):
            load_a_scales(q)
        for g in range(KG):
            load_b(3, g)

        banks = {}

        def turn_x(i):
            words = x_sb[:, i, :].bitcast(F32)
            banks["x", i] = bank_u("x%d" % i, [P, KG, 2, P])
            for g in range(KG):
                for u in range(2):
                    nc.tensor.transpose(
                        banks["x", i][:, g, u, :], words[:, 256 * g + u : 256 * (g + 1) : 2], ident[:]
                    )

        def take_x(i):
            dst = x_in[:, i, :, :, :].rearrange("p g n t -> p (g n t)").bitcast(F32)
            nc.scalar.copy(
                out=dst.rearrange("p (g n u) -> p g n u", g=KG, u=2),
                in_=banks["x", i][:].rearrange("p g u n -> p g n u"),
            )

        def quant_x(i):
            nc.vector.quantize_mx(
                out=x_codes[:, i, :, :].rearrange("p g n -> p (g n)").bitcast(FP8X4),
                scales=x_scales[:, i, :, :].rearrange("p g n -> p (g n)"),
                in_=x_in[:, i, :, :, :].rearrange("p g n t -> p (g n t)"),
            )

        def turn_vectors():
            banks["v"] = bank_u("v", [P, 5, P], BF16)
            for t in range(4):
                nc.tensor.transpose(banks["v"][:, t, :], vectors[:, t:R:4], ident_b[:])
            nc.tensor.transpose(banks["v"][:, 4, :], vectors[:, R : R + P], ident_b[:])

        def take_vectors():
            nc.scalar.copy(
                out=lam_t[:].rearrange("p m o t -> p m (o t)"),
                in_=banks["v"][:, 0:4, 0:NB].rearrange("p t m -> p m t"),
            )
            nc.scalar.copy(out=gam_t[:], in_=banks["v"][:, 4, 0 : NB * NJ])

        def lay_out_b(m, g, c0, c1, copy):
            dst = b_in[m][:, g, :].rearrange("p (t c i k) -> p c t i k", t=4, i=2, k=4)
            src = b_sb[m][:, g, :, :].rearrange("p k (c i t) -> p c t i k", i=2, t=4)
            copy(out=dst[:, c0:c1], in_=src[:, c0:c1])

        def quant_b(m, g0, g1):
            nc.vector.quantize_mx(
                out=b_codes[m][:, g0:g1, :].rearrange("p g r -> p (g r)").bitcast(FP8X4),
                scales=b_scales[m][:, g0:g1, :].rearrange("p g r -> p (g r)"),
                in_=b_in[m][:, g0:g1, :].rearrange("p g r -> p (g r)"),
            )

        def stage1(m, i):
            banks["h", m, i] = bank_h("h%d_%d" % (m, i), [P, 4, P])
            for t in range(4):
                cols = slice(P * t, P * (t + 1))
                for g in range(KG):
                    nc.tensor.matmul_mx(
                        out=banks["h", m, i][:, t, :],
                        lhsT=b_codes[m][:, g, cols].bitcast(FP8X4),
                        lhsT_scale=b_scales[m][:, g, cols],
                        rhs=x_codes[:, i, g, :].bitcast(FP8X4),
                        rhs_scale=x_scales[:, i, g, :],
                        start=(g == 0),
                        stop=(g == KG - 1),
                    )

        def scale_h(m, i):
            nc.vector.tensor_tensor(
                out=hl[m][:, P * i : P * (i + 1), :],
                in0=banks["h", m, i][:].rearrange("p t n -> p n t"),
                in1=lam_t[:, m, :, :].to_broadcast([P, P, 4]),
                op=MULT,
            )

        def quant_h(m):
            nc.vector.quantize_mx(
                out=h_codes[m][:].bitcast(FP8X4),
                scales=h_scales[m][:],
                in_=hl[m][:].rearrange("p n t -> p (n t)"),
            )

        def base(j):
            banks["base", j] = bank_u("base%d" % j, [P, TOK])
            for i in range(NT):
                for g in range(KG):
                    nc.tensor.matmul_mx(
                        out=banks["base", j][:, P * i : P * (i + 1)],
                        lhsT=w0_sb[:, g, 256 * j : 256 * (j + 1)].bitcast(FP4X4),
                        lhsT_scale=w_scales[:, g, P * j : P * (j + 1)],
                        rhs=x_codes[:, i, g, :].bitcast(FP8X4),
                        rhs_scale=x_scales[:, i, g, :],
                        start=(g == 0),
                        stop=(g == KG - 1),
                    )

        def take_base(j):
            nc.scalar.copy(out=acc[:, j, :], in_=banks["base", j][:])

        def stage2(m, j):
            banks["u", m, j] = bank_u("u%d_%d" % (m, j), [P, TOK])
            nc.tensor.matmul_mx(
                out=banks["u", m, j][:],
                lhsT=a_sb[:, 256 * j : 256 * (j + 1)].bitcast(FP4X4),
                lhsT_scale=w_scales[:, KG, P * j : P * (j + 1)],
                rhs=h_codes[m][:].bitcast(FP8X4),
                rhs_scale=h_scales[m][:],
                start=True,
                stop=True,
            )

        def take_u(m, j):
            gam_col = gam_t[:, NJ * m + j : NJ * m + j + 1]
            if (m, j) in SCALAR_U:
                nc.scalar.activation(out=scaled[m, j][:], in_=banks["u", m, j][:], func=COPY, scale=gam_col)
            else:
                nc.vector.scalar_tensor_tensor(
                    out=acc[:, j, :], in0=banks["u", m, j][:], scalar=gam_col, in1=acc[:, j, :], op0=MULT, op1=ADD
                )

        def add_u(m, j):
            nc.gpsimd.tensor_tensor(out=acc[:, j, :], in0=acc[:, j, :], in1=scaled[m, j][:], op=ADD)

        def turn_out(j):
            banks["o", j] = bank_h("o%d" % j, [P, NT, P])
            parts = [scaled[mj][:] for mj in sorted(TENSOR_ADDS) if mj[1] == j] + [acc[:, j, :]]
            for i in range(NT):
                for n, part in enumerate(parts):
                    nc.tensor.matmul(
                        banks["o", j][:, i, :],
                        lhsT=part[:, P * i : P * (i + 1)],
                        rhs=ident[:],
                        start=(n == 0),
                        stop=(n == len(parts) - 1),
                        is_transpose=True,
                    )

        def take_out(j):
            nc.scalar.copy(out=o32[:, :, P * j : P * (j + 1)], in_=banks["o", j][:])

        def store(j0, j1):
            cols = slice(P * j0, P * j1)
            nc.sync.dma_start(out=out_0[:, cols].rearrange("(i p) f -> p i f", p=P), in_=o32[:, :, cols])

        def round_out(j0, j1):
            cols = slice(P * j0, P * j1)
            nc.vector.tensor_copy(out=o16[:, :, cols], in_=o32[:, :, cols])

        def turn_plane(h, half):
            banks["p", h, half] = bank_h("p%d_%d" % (h, half), [P, 2, 2, P])
            for ii in range(2):
                words = o16[:, 2 * half + ii, :].bitcast(F32)
                for u in range(2):
                    nc.tensor.transpose(
                        banks["p", h, half][:, ii, u, :], words[:, 256 * h + u : 256 * (h + 1) : 2], ident[:]
                    )

        def take_plane(h, half):
            dst = p_in[:, h, 256 * half : 256 * (half + 1), :].rearrange("p n t -> p (n t)").bitcast(F32)
            nc.scalar.copy(
                out=dst.rearrange("p (i n u) -> p i n u", i=2, u=2),
                in_=banks["p", h, half][:].rearrange("p i u n -> p i n u"),
            )

        def quant_plane(h, n0, n1):
            nc.vector.quantize_mx(
                out=p_codes[:, h, n0:n1].bitcast(FP8X4),
                scales=p_scales[:, h, n0:n1],
                in_=p_in[:, h, n0:n1, :].rearrange("p n t -> p (n t)"),
            )
            words = out_1[h].rearrange("p n t -> p (n t)").bitcast(I32)
            nc.sync.dma_start(out=words[:, n0:n1], in_=p_codes[:, h, n0:n1].bitcast(I32))

        def store_scales(h):
            for q in range(4):
                queue = nc.sync if q % 2 == 0 else nc.scalar
                queue.dma_start(
                    out=out_2[h, 4 * q : 4 * q + 4, :].bitcast(I32),
                    in_=p_scales[32 * q : 32 * q + 4, h, :].bitcast(I32),
                )

        steps = {}

        def step(name, engine, weight, after, fn, args, takes=None, frees=None, at=0):
            steps[name] = (engine, weight, after, takes, frees, at, fn, args)

        read = WEIGHT["read"]
        for i in range(NT):
            step(("turn_x", i), "T", WEIGHT["turn_x"], [], turn_x, (i,), takes="u", at=ARRIVE_X[i])
            step(("take_x", i), "S", WEIGHT["take_x"], [("turn_x", i)], take_x, (i,), frees="u")
            step(("quant_x", i), "V", WEIGHT["quant_x"], [("take_x", i)], quant_x, (i,))
        step(("turn_vectors",), "T", WEIGHT["turn_vectors"], [], turn_vectors, (), takes="u", at=ARRIVE_VECTORS)
        step(("take_vectors",), "S", WEIGHT["take_vectors"], [("turn_vectors",)], take_vectors, (), frees="u")
        for m in range(NB):
            laid = []
            for g in range(KG):
                cut = VECTOR_SHARE[m][g]
                if cut > 0:
                    args = (m, g, 0, cut, nc.vector.tensor_copy)
                    step(("lay_v", m, g), "V", (35 * cut) // 100 + 2, [], lay_out_b, args, at=ARRIVE_B[m][g])
                    laid.append(("lay_v", m, g))
                if cut < 64:
                    args = (m, g, cut, 64, nc.scalar.copy)
                    step(("lay_s", m, g), "S", (64 * (64 - cut)) // 100 + 2, [], lay_out_b, args, at=ARRIVE_B[m][g])
                    laid.append(("lay_s", m, g))
                if m == 0:
                    step(("quant_b", m, g), "V", WEIGHT["quant_half"], laid, quant_b, (m, g, g + 1))
                    laid = []
            quantised = [("quant_b", 0, 0), ("quant_b", 0, 1)]
            if m > 0:
                step(("quant_b", m), "V", WEIGHT["quant_whole"], laid, quant_b, (m, 0, KG))
                quantised = [("quant_b", m)]
            for i in range(NT):
                step(("stage1", m, i), "T", WEIGHT["stage1"], quantised + [("quant_x", i)], stage1, (m, i), takes="h")
                after = [("stage1", m, i), ("take_vectors",)]
                step(("scale", m, i), "V", read, after, scale_h, (m, i), frees="h")
            step(("quant_h", m), "V", WEIGHT["quant_h"], [("scale", m, i) for i in range(NT)], quant_h, (m,))
        for j in range(NJ):
            after = [("quant_x", i) for i in range(NT)]
            step(("base", j), "T", WEIGHT["base"], after, base, (j,), takes="u", at=ARRIVE_W0)
            step(("take_base", j), "S", read, [("base", j)], take_base, (j,), frees="u")
            for m in range(NB):
                step(("stage2", m, j), "T", WEIGHT["stage2"], [("quant_h", m)], stage2, (m, j), takes="u", at=ARRIVE_A)
            last = ("take_base", j)
            for m in (3, 0, 1, 2) if j == FIRST_ADD[1] else range(NB):
                if (m, j) in SCALAR_U:
                    step(("take_u", m, j), "S", read, [("stage2", m, j)], take_u, (m, j), frees="u")
                if (m, j) in GPSIMD_ADDS:
                    after = [("take_u", m, j), last] + ([("add",) + FIRST_ADD] if (m, j) != FIRST_ADD else [])
                    step(("add", m, j), "G", WEIGHT["add"], after, add_u, (m, j))
                    last = ("add", m, j)
                elif (m, j) not in SCALAR_U:
                    step(("take_u", m, j), "V", read, [("stage2", m, j), last], take_u, (m, j), frees="u")
                    last = ("take_u", m, j)
            apart = [("take_u",) + mj for mj in sorted(TENSOR_ADDS) if mj[1] == j]
            weight = WEIGHT["out"] * (1 + len(apart))
            step(("turn_out", j), "T", weight, apart + [last], turn_out, (j,), takes="h")
            step(("take_out", j), "S", read, [("turn_out", j)], take_out, (j,), frees="h")
        for j in range(0, NJ, 2):
            pair = [("take_out", j), ("take_out", j + 1)]
            step(("store", j), "D", WEIGHT["store"], pair, store, (j, j + 2))
            if j < NJ // 2:
                step(("round", j), "V", WEIGHT["round_two"], pair, round_out, (j, j + 2))
            else:
                for jj in (j, j + 1):
                    step(("round", jj), "V", WEIGHT["round_one"], [("take_out", jj)], round_out, (jj, jj + 1))
        for h in range(2):
            rounded = [n for n in steps if n[0] == "round" and n[1] // 4 == h]
            for half in range(2):
                step(("turn_plane", h, half), "T", WEIGHT["turn_plane"], rounded, turn_plane, (h, half), takes="h")
                step(("take_plane", h, half), "S", read, [("turn_plane", h, half)], take_plane, (h, half), frees="h")
            if h == 0:
                taken = [("take_plane", 0, 0), ("take_plane", 0, 1)]
                step(("quant_plane", 0), "V", WEIGHT["quant_plane"], taken, quant_plane, (0, 0, TOK))
            else:
                for half in range(2):
                    args = (1, 256 * half, 256 * (half + 1))
                    after = [("take_plane", 1, half)]
                    step(("quant_plane", 1, half), "V", WEIGHT["quant_half_plane"], after, quant_plane, args)
            done = [n for n in steps if n[0] == "quant_plane" and n[1] == h]
            step(("store_scales", h), "D", WEIGHT["store"], done, store_scales, (h,))

        def list_order():
            followers = {n: [] for n in steps}
            for n in steps:
                for before in steps[n][2]:
                    followers[before].append(n)
            way = {}
            for n in steps:
                stack = [n]
                while stack:
                    open_followers = [f for f in followers[stack[-1]] if f not in way]
                    if open_followers:
                        stack.extend(open_followers)
                    else:
                        top = stack.pop()
                        way[top] = steps[top][1] + HOP + max([way[f] for f in followers[top]] + [0])
            clock = {e: 0 for e in "TVSGD"}
            free = {"h": [0] * BANKS_H, "u": [0] * BANKS_U}
            ready = {n: steps[n][5] for n in steps}
            waits = {n: len(steps[n][2]) for n in steps}
            startable = [n for n in steps if waits[n] == 0]
            order, turned_before = [], None
            while startable:
                choice = None
                for e in clock:
                    starts = []
                    for n in startable:
                        takes = steps[n][3]
                        if steps[n][0] == e and (takes is None or free[takes]):
                            starts.append((max(clock[e], ready[n], min(free[takes]) if takes else 0), n))
                    if starts:
                        soonest = min([t for t, n in starts])
                        rank = max([(way[n] + BIAS.get(n[0], 0), str(n), n) for t, n in starts if t == soonest])
                        if choice is None or soonest < choice[0]:
                            choice = (soonest, rank[2])
                t, n = choice
                engine, weight, after, takes, frees = steps[n][:5]
                if takes:
                    free[takes].remove(min(free[takes]))
                if engine == "T":
                    turned = n[0].startswith("turn")
                    t += SWITCH if turned_before not in (None, turned) else 0
                    turned_before = turned
                clock[engine] = t + weight
                if frees:
                    free[frees].append(t + weight + LAG)
                startable.remove(n)
                order.append(n)
                for f in followers[n]:
                    lag = TENSOR_LAG if engine == "T" else LAG
                    if steps[f][0] == engine:
                        lag = VECTOR_LAG if engine == "V" else 0
                    ready[f] = max(ready[f], t + weight + lag)
                    waits[f] -= 1
                    if waits[f] == 0:
                        startable.append(f)
            return order

        with tc.manual_schedule():
            for n in list_order():
                steps[n][6](*steps[n][7])
